import numpy as np
import ml_dtypes


def mxq(x, axis, fmt="e4m3"):
    dtype, down = {"e4m3": (ml_dtypes.float8_e4m3fn, 7), "e5m2": (ml_dtypes.float8_e5m2, 14)}[fmt]
    v = np.moveaxis(np.asarray(x, np.float32).astype(ml_dtypes.bfloat16).astype(np.float64), axis, -1)
    blocks = v.reshape(v.shape[:-1] + (-1, 32))
    amax = np.abs(blocks).max(-1, keepdims=True)
    byte = np.maximum(np.where(amax > 0, np.frexp(amax)[1] - 1 + 127, 0) - down, 1)
    scale = np.exp2(byte - 127.0)
    codes = (blocks / scale).astype(np.float32).astype(dtype).astype(np.float64)
    return np.moveaxis((codes * scale).reshape(v.shape), -1, axis)


WIDE = False


def mx_kscale(k):
    if not WIDE:
        return np.ones(k)
    levels = np.array([10, -10, 5, -5, 0])
    if k % 512:
        return np.exp2(np.random.permutation(np.resize(levels, k // 32))).repeat(32)
    a = np.empty((k // 512, 16))
    for p in range(k // 512):
        a[p, :8] = np.random.permutation(np.resize(levels, 8))
        for g in range(8):
            far = levels[np.abs(levels - a[p, g]) >= 10]
            a[p, g + 8] = far[np.random.randint(len(far))]
    return np.exp2(a.ravel()).repeat(32)


def f64(x):
    return np.asarray(x).astype(np.float64)


def striped(idx):
    return np.tile(idx.reshape(-1, 16).T, (8, 1)).astype(np.uint16)


def unstriped(offs):
    return offs[:16].T.reshape(-1).astype(np.int64)


E2M1 = np.array([0.0, 0.5, 1.0, 1.5, 2.0, 3.0, 4.0, 6.0, -0.0, -0.5, -1.0, -1.5, -2.0, -3.0, -4.0, -6.0])


def pack_fp4(w):
    k, n = w.shape
    w = f64(np.asarray(w, np.float32).astype(ml_dtypes.bfloat16)).reshape(k // 32, 32, n)
    amax = np.abs(w).max(1)
    mant, ex = np.frexp(amax / 6.0)
    byte = np.clip(np.where(amax > 0, np.where(mant > 0.5, ex, ex - 1) + 127, 1), 1, 254)
    scaled = (w * np.exp2(127.0 - byte)[:, None, :]).reshape(k, n).astype(np.float32)
    c = np.ascontiguousarray(scaled.reshape(k // 512, 128, 4, n).transpose(0, 1, 3, 2)).astype(ml_dtypes.float4_e2m1fn).view(np.uint8) & 0xF
    words = (c[..., 0::2] | (c[..., 1::2] << 4)).reshape(k // 512, 128, 2 * n)
    return np.ascontiguousarray(words), np.ascontiguousarray(byte.astype(np.uint8).reshape(k // 512, 16, n))


def unpack_fp4(words, scales):
    g, _, n = scales.shape
    words = np.ascontiguousarray(words).reshape(g, 128, n, 2)
    nib = np.empty((g, 128, n, 4), np.uint8)
    nib[..., 0::2] = words & 0xF
    nib[..., 1::2] = words >> 4
    vals = E2M1[nib] * np.repeat(np.exp2(scales.astype(np.float64) - 127.0), 8, axis=1)[..., None]
    return vals.transpose(0, 1, 3, 2).reshape(g * 512, n)


def sigmoid(v):
    return 1.0 / (1.0 + np.exp(-np.maximum(v, -700.0)))


K, T, S, N, U = 512, 2048, 1024, 128, 2048


def setup_inputs():
    n = np.random.standard_normal
    s = mx_kscale(K)[:, None]
    packed_w1 = pack_fp4(n((K, N)) / np.sqrt(K) / s)
    packed_w2 = pack_fp4(n((K, N)) / np.sqrt(K) / s)
    return {
        "xT": (n((K, T)) * s).astype(np.float32),
        "mem": n((N, U)).astype(np.float32),
        "w1_words": packed_w1[0],
        "w1_scales": packed_w1[1],
        "w2_words": packed_w2[0],
        "w2_scales": packed_w2[1],
        "offs": striped(np.random.permutation(T)[:S]),
        "slot": striped(np.random.permutation(U)[:S]),
    }


def reference(xT, mem, w1_words, w1_scales, w2_words, w2_scales, offs, slot):
    old = f64(mem)[:, unstriped(slot)]
    xq = mxq(f64(xT)[:, unstriped(offs)], 0, "e4m3")
    g = sigmoid(unpack_fp4(w2_words, w2_scales).T @ xq)
    y = np.tanh(unpack_fp4(w1_words, w1_scales).T @ xq)
    out = f64(mem).copy()
    out[:, unstriped(slot)] = old + g * (y - old)
    return out

@@ -1,0 +1,146 @@
+from contextlib import ExitStack
+
+import concourse.mybir as mybir
+
+K, T, S, N, U = 512, 2048, 1024, 128, 2048
+FLOPS = 2 * 2 * K * N * S
+
+F32 = mybir.dt.float32
+BF16 = mybir.dt.bfloat16
+I32 = mybir.dt.int32
+U32 = mybir.dt.uint32
+U16 = mybir.dt.uint16
+U8 = mybir.dt.uint8
+FP8X4 = mybir.dt.float8_e4m3fn_x4
+FP4X4 = mybir.dt.float4_e2m1fn_x4
+ACT = mybir.ActivationFunctionType
+ALU = mybir.AluOpType
+
+P = 128
+CH = 256
+NCH = S // CH
+LOADS = ((1024, 1024), (1024, 512, 512))
+
+
+def tile_picked_gmem_tanh_e_kernel(tc, xT, mem, w1_words, w1_scales, w2_words, w2_scales, offs, slot, out):
+    nc = tc.nc
+    with ExitStack() as ctx:
+        sb = ctx.enter_context(tc.tile_pool(name="sb", bufs=1))
+        ps = ctx.enter_context(tc.psum_pool(name="ps", bufs=1))
+
+        offs_sb = sb.tile([P, S // 16], U16, name="offs_sb")
+        slot_sb = sb.tile([P, S // 16], U16, name="slot_sb")
+        memory = sb.tile([P, U], F32, name="memory")
+        x_rows = xT.rearrange("(p j) t -> p j t", j=4)
+
+        raw = []
+        for u in range(2):
+            t0 = 0
+            for i, w in enumerate(LOADS[u]):
+                tile = sb.tile([P, 2, w], F32, name="raw%d_%d" % (u, i))
+                nc.sync.dma_start(out=tile[:], in_=x_rows[:, 2 * u : 2 * u + 2, t0 : t0 + w])
+                raw.append((u, t0, w, tile))
+                t0 = t0 + w
+            if u == 0:
+                nc.sync.dma_start(offs_sb[:], offs)
+        nc.sync.dma_start(out=memory[:], in_=mem)
+        nc.sync.dma_start(slot_sb[:], slot)
+
+        w_words = []
+        w_scales = sb.tile([P, 2 * N], U8, name="w_scales", align_bytes=64)
+        nc.gpsimd.memset(w_scales[:].bitcast(I32), 0)
+        for i, (words, scales) in enumerate(((w1_words, w1_scales), (w2_words, w2_scales))):
+            tile = sb.tile([P, 2 * N], U8, name="w_words%d" % i, align_bytes=64)
+            nc.scalar.dma_start(out=tile[:].bitcast(I32), in_=words[0].bitcast(I32))
+            w_words.append(tile)
+            for q in range(4):
+                (nc.scalar if i == 0 else nc.gpsimd).dma_start(
+                    out=w_scales[32 * q : 32 * q + 4, i * N : (i + 1) * N].bitcast(I32),
+                    in_=scales[0, 4 * q : 4 * q + 4, :].bitcast(I32),
+                )
+
+        pairs = [sb.tile([P, T, 2], BF16, name="pairs%d" % u) for u in range(2)]
+        windows = [pairs[u][:].rearrange("p t e -> p (t e)").bitcast(U32) for u in range(2)]
+
+        def cast(engine_copy, u, t0, tile, a, b):
+            engine_copy(out=pairs[u][:, t0 + a : t0 + b, :], in_=tile[:, :, a:b].rearrange("p e t -> p t e"))
+
+        def entries(lst, a, b):
+            return lst[:, a // 16 : b // 16]
+
+        grouped = [sb.tile([P, CH, 2], U32, name="grouped%d" % c, align_bytes=64) for c in range(NCH)]
+        halves = [sb.tile([P, 2, CH], U32, name="halves%d" % c) for c in range(NCH)]
+
+        def gather(u, c):
+            dst = halves[c][:, u, :]
+            nc.vector.tensor_copy(out=dst, in_=windows[u].indirect(entries(offs_sb, c * CH, (c + 1) * CH)))
+
+        def cast_shared(i, split):
+            u, t0, w, tile = raw[i]
+            if split > 0:
+                cast(nc.vector.tensor_copy, u, t0, tile, 0, split)
+            if split < w:
+                cast(nc.scalar.copy, u, t0, tile, split, w)
+
+        cast_shared(0, 1024)
+        cast_shared(1, 704)
+        for c in range(NCH):
+            gather(0, c)
+        cast_shared(2, 256)
+        cast_shared(3, 512)
+        cast_shared(4, 352)
+
+        cand = sb.tile([P, S], F32, name="cand")
+        keep = sb.tile([P, S], F32, name="keep")
+        diff = sb.tile([P, S], F32, name="diff")
+        step = sb.tile([P, S], F32, name="step")
+
+        def weave(c):
+            nc.scalar.copy(out=grouped[c][:], in_=halves[c][:].rearrange("p u n -> p n u"))
+
+        def products(c):
+            codes = sb.tile([P, CH], U32, name="codes%d" % c, align_bytes=64)
+            scales = sb.tile([P, CH], U8, name="scales%d" % c, align_bytes=64)
+            nc.vector.quantize_mx(
+                out=codes[:].bitcast(FP8X4),
+                scales=scales[:],
+                in_=grouped[c][:].rearrange("p n u -> p (n u)").bitcast(BF16),
+            )
+            cols = slice(c * CH, (c + 1) * CH)
+            for i, dst, func, scale in ((1, keep, ACT.Sigmoid, -1.0), (0, cand, ACT.Tanh, 1.0)):
+                acc = ps.tile([P, CH], F32, name="acc%d_%d" % (c, i))
+                nc.tensor.matmul_mx(
+                    out=acc[:],
+                    lhsT=w_words[i][:].bitcast(FP4X4),
+                    lhsT_scale=w_scales[:, i * N : (i + 1) * N],
+                    rhs=codes[:].bitcast(FP8X4),
+                    rhs_scale=scales[:],
+                    start=True,
+                    stop=True,
+                )
+                nc.scalar.activation(out=dst[:, cols], in_=acc[:], func=func, scale=scale)
+
+        def subtract(c):
+            cols = slice(c * CH, (c + 1) * CH)
+            nc.vector.tensor_tensor(diff[:, cols], memory[:].indirect(entries(slot_sb, cols.start, cols.stop)), cand[:, cols], ALU.subtract)
+
+        def scale_diff(a, b):
+            nc.vector.tensor_tensor(step[:, a:b], diff[:, a:b], keep[:, a:b], ALU.mult)
+
+        def scatter(a, b):
+            nc.vector.tensor_tensor(memory[:].indirect(entries(slot_sb, a, b)), step[:, a:b], cand[:, a:b], ALU.add)
+
+        for c in range(NCH):
+            gather(1, c)
+            weave(c)
+        for c in range(NCH):
+            products(c)
+        subtract(0)
+        subtract(1)
+        scale_diff(0, 512)
+        subtract(2)
+        subtract(3)
+        scatter(0, 512)
+        scale_diff(512, 1024)
+        scatter(512, 1024)
+        nc.sync.dma_start(out=out, in_=memory[:])

@@ -46,6 +46,10 @@ def tile_picked_gmem_tanh_e_kernel(tc, xT, mem, w1_words, w1_scales, w2_words, w
         nc.sync.dma_start(out=memory[:], in_=mem)
         nc.sync.dma_start(slot_sb[:], slot)
 
+        warm = sb.tile([P, 2], F32, name="warm")
+        nc.vector.memset(warm[:, 0:1], 0.0)
+        nc.scalar.activation(out=warm[:, 1:2], in_=warm[:, 0:1], func=ACT.Sigmoid)
+
         w_words = []
         w_scales = sb.tile([P, 2 * N], U8, name="w_scales", align_bytes=64)
         nc.gpsimd.memset(w_scales[:].bitcast(I32), 0)

@@ -19,7 +19,14 @@ ALU = mybir.AluOpType
 P = 128
 CH = 256
 NCH = S // CH
-LOADS = ((1024, 1024), (1024, 512, 512))
+LOADS = (
+    ((0, 1, 0, 2048), (1, 1, 0, 1280), (1, 1, 1280, 2048)),
+    ((0, 2, 0, 1024), (0, 1, 1024, 2048), (1, 1, 1024, 1536), (1, 1, 1536, 2048)),
+)
+CASTS = (
+    ((0, 800, 1280), (1280, 1760, 2048)),
+    ((0, 512, 1024), (1024, 1344, 1536), (1536, 1856, 2048)),
+)
 
 
 def tile_picked_gmem_tanh_e_kernel(tc, xT, mem, w1_words, w1_scales, w2_words, w2_scales, offs, slot, out):
@@ -33,16 +40,17 @@ def tile_picked_gmem_tanh_e_kernel(tc, xT, mem, w1_words, w1_scales, w2_words, w
         memory = sb.tile([P, U], F32, name="memory")
         x_rows = xT.rearrange("(p j) t -> p j t", j=4)
 
-        raw = []
+        raw = [sb.tile([P, 2, T], F32, name="raw%d" % u) for u in range(2)]
         for u in range(2):
-            t0 = 0
-            for i, w in enumerate(LOADS[u]):
-                tile = sb.tile([P, 2, w], F32, name="raw%d_%d" % (u, i))
-                nc.sync.dma_start(out=tile[:], in_=x_rows[:, 2 * u : 2 * u + 2, t0 : t0 + w])
-                raw.append((u, t0, w, tile))
-                t0 = t0 + w
+            for e, n, a, b in LOADS[u]:
+                nc.sync.dma_start(out=raw[u][:, e : e + n, a:b], in_=x_rows[:, 2 * u + e : 2 * u + e + n, a:b])
             if u == 0:
                 nc.sync.dma_start(offs_sb[:], offs)
+        w_words = []
+        for i, words in enumerate((w1_words, w2_words)):
+            tile = sb.tile([P, 2 * N], U8, name="w_words%d" % i, align_bytes=64)
+            nc.sync.dma_start(out=tile[:].bitcast(I32), in_=words[0].bitcast(I32))
+            w_words.append(tile)
         nc.sync.dma_start(out=memory[:], in_=mem)
         nc.sync.dma_start(slot_sb[:], slot)
 
@@ -50,15 +58,11 @@ def tile_picked_gmem_tanh_e_kernel(tc, xT, mem, w1_words, w1_scales, w2_words, w
         nc.vector.memset(warm[:, 0:1], 0.0)
         nc.scalar.activation(out=warm[:, 1:2], in_=warm[:, 0:1], func=ACT.Sigmoid)
 
-        w_words = []
         w_scales = sb.tile([P, 2 * N], U8, name="w_scales", align_bytes=64)
         nc.gpsimd.memset(w_scales[:].bitcast(I32), 0)
-        for i, (words, scales) in enumerate(((w1_words, w1_scales), (w2_words, w2_scales))):
-            tile = sb.tile([P, 2 * N], U8, name="w_words%d" % i, align_bytes=64)
-            nc.scalar.dma_start(out=tile[:].bitcast(I32), in_=words[0].bitcast(I32))
-            w_words.append(tile)
+        for i, scales in enumerate((w1_scales, w2_scales)):
             for q in range(4):
-                (nc.scalar if i == 0 else nc.gpsimd).dma_start(
+                nc.gpsimd.dma_start(
                     out=w_scales[32 * q : 32 * q + 4, i * N : (i + 1) * N].bitcast(I32),
                     in_=scales[0, 4 * q : 4 * q + 4, :].bitcast(I32),
                 )
@@ -66,8 +70,10 @@ def tile_picked_gmem_tanh_e_kernel(tc, xT, mem, w1_words, w1_scales, w2_words, w
         pairs = [sb.tile([P, T, 2], BF16, name="pairs%d" % u) for u in range(2)]
         windows = [pairs[u][:].rearrange("p t e -> p (t e)").bitcast(U32) for u in range(2)]
 
-        def cast(engine_copy, u, t0, tile, a, b):
-            engine_copy(out=pairs[u][:, t0 + a : t0 + b, :], in_=tile[:, :, a:b].rearrange("p e t -> p t e"))
+        def cast(u):
+            for first, split, end in CASTS[u]:
+                for copy, a, b in ((nc.vector.tensor_copy, first, split), (nc.scalar.copy, split, end)):
+                    copy(out=pairs[u][:, a:b, :], in_=raw[u][:, :, a:b].rearrange("p e t -> p t e"))
 
         def entries(lst, a, b):
             return lst[:, a // 16 : b // 16]
@@ -79,20 +85,10 @@ def tile_picked_gmem_tanh_e_kernel(tc, xT, mem, w1_words, w1_scales, w2_words, w
             dst = halves[c][:, u, :]
             nc.vector.tensor_copy(out=dst, in_=windows[u].indirect(entries(offs_sb, c * CH, (c + 1) * CH)))
 
-        def cast_shared(i, split):
-            u, t0, w, tile = raw[i]
-            if split > 0:
-                cast(nc.vector.tensor_copy, u, t0, tile, 0, split)
-            if split < w:
-                cast(nc.scalar.copy, u, t0, tile, split, w)
-
-        cast_shared(0, 1024)
-        cast_shared(1, 704)
+        cast(0)
         for c in range(NCH):
             gather(0, c)
-        cast_shared(2, 256)
-        cast_shared(3, 512)
-        cast_shared(4, 352)
+        cast(1)
 
         cand = sb.tile([P, S], F32, name="cand")
         keep = sb.tile([P, S], F32, name="keep")
@@ -102,27 +98,28 @@ def tile_picked_gmem_tanh_e_kernel(tc, xT, mem, w1_words, w1_scales, w2_words, w
         def weave(c):
             nc.scalar.copy(out=grouped[c][:], in_=halves[c][:].rearrange("p u n -> p n u"))
 
-        def products(c):
-            codes = sb.tile([P, CH], U32, name="codes%d" % c, align_bytes=64)
-            scales = sb.tile([P, CH], U8, name="scales%d" % c, align_bytes=64)
+        codes = sb.tile([P, S], U32, name="codes", align_bytes=64)
+        scales = sb.tile([P, S], U8, name="scales", align_bytes=64)
+
+        def quantise(c):
             nc.vector.quantize_mx(
-                out=codes[:].bitcast(FP8X4),
-                scales=scales[:],
+                out=codes[:, c * CH : (c + 1) * CH].bitcast(FP8X4),
+                scales=scales[:, c * CH : (c + 1) * CH],
                 in_=grouped[c][:].rearrange("p n u -> p (n u)").bitcast(BF16),
             )
-            cols = slice(c * CH, (c + 1) * CH)
-            for i, dst, func, scale in ((1, keep, ACT.Sigmoid, -1.0), (0, cand, ACT.Tanh, 1.0)):
-                acc = ps.tile([P, CH], F32, name="acc%d_%d" % (c, i))
-                nc.tensor.matmul_mx(
-                    out=acc[:],
-                    lhsT=w_words[i][:].bitcast(FP4X4),
-                    lhsT_scale=w_scales[:, i * N : (i + 1) * N],
-                    rhs=codes[:].bitcast(FP8X4),
-                    rhs_scale=scales[:],
-                    start=True,
-                    stop=True,
-                )
-                nc.scalar.activation(out=dst[:, cols], in_=acc[:], func=func, scale=scale)
+
+        def product(i, a, b, dst, func, scale):
+            acc = ps.tile([P, b - a], F32, name="acc%d_%d" % (i, a))
+            nc.tensor.matmul_mx(
+                out=acc[:],
+                lhsT=w_words[i][:].bitcast(FP4X4),
+                lhsT_scale=w_scales[:, i * N : (i + 1) * N],
+                rhs=codes[:, a:b].bitcast(FP8X4),
+                rhs_scale=scales[:, a:b],
+                start=True,
+                stop=True,
+            )
+            nc.scalar.activation(out=dst[:, a:b], in_=acc[:], func=func, scale=scale)
 
         def subtract(c):
             cols = slice(c * CH, (c + 1) * CH)
@@ -138,13 +135,14 @@ def tile_picked_gmem_tanh_e_kernel(tc, xT, mem, w1_words, w1_scales, w2_words, w
             gather(1, c)
             weave(c)
         for c in range(NCH):
-            products(c)
-        subtract(0)
-        subtract(1)
+            quantise(c)
+        for c in range(NCH):
+            product(0, c * CH, (c + 1) * CH, cand, ACT.Tanh, 1.0)
+        for a in (0, 512):
+            product(1, a, a + 512, keep, ACT.Sigmoid, -1.0)
+        for c in range(NCH):
+            subtract(c)
         scale_diff(0, 512)
-        subtract(2)
-        subtract(3)
-        scatter(0, 512)
         scale_diff(512, 1024)
-        scatter(512, 1024)
+        scatter(0, 1024)
         nc.sync.dma_start(out=out, in_=memory[:])

@@ -21,11 +21,11 @@ CH = 256
 NCH = S // CH
 LOADS = (
     ((0, 1, 0, 2048), (1, 1, 0, 1280), (1, 1, 1280, 2048)),
-    ((0, 2, 0, 1024), (0, 1, 1024, 2048), (1, 1, 1024, 1536), (1, 1, 1536, 2048)),
+    ((0, 2, 0, 1024), (0, 1, 1024, 2048), (1, 1, 1024, 1664), (1, 1, 1664, 2048)),
 )
 CASTS = (
     ((0, 800, 1280), (1280, 1760, 2048)),
-    ((0, 512, 1024), (1024, 1344, 1536), (1536, 1856, 2048)),
+    ((0, 512, 1024), (1024, 1424, 1664), (1664, 1904, 2048)),
 )
 
 
@@ -46,26 +46,26 @@ def tile_picked_gmem_tanh_e_kernel(tc, xT, mem, w1_words, w1_scales, w2_words, w
                 nc.sync.dma_start(out=raw[u][:, e : e + n, a:b], in_=x_rows[:, 2 * u + e : 2 * u + e + n, a:b])
             if u == 0:
                 nc.sync.dma_start(offs_sb[:], offs)
-        w_words = []
-        for i, words in enumerate((w1_words, w2_words)):
-            tile = sb.tile([P, 2 * N], U8, name="w_words%d" % i, align_bytes=64)
-            nc.sync.dma_start(out=tile[:].bitcast(I32), in_=words[0].bitcast(I32))
-            w_words.append(tile)
+        w_words = [sb.tile([P, 2 * N], U8, name="w_words%d" % i, align_bytes=64) for i in range(2)]
+        w_scales = sb.tile([P, 2 * N], U8, name="w_scales", align_bytes=64)
+        nc.vector.memset(w_scales[:].bitcast(I32), 0)
+
+        def load_weights(i, words, scales):
+            nc.sync.dma_start(out=w_words[i][:].bitcast(I32), in_=words[0].bitcast(I32))
+            for q in range(4):
+                nc.sync.dma_start(
+                    out=w_scales[32 * q : 32 * q + 4, i * N : (i + 1) * N].bitcast(I32),
+                    in_=scales[0, 4 * q : 4 * q + 4, :].bitcast(I32),
+                )
+
+        load_weights(0, w1_words, w1_scales)
         nc.sync.dma_start(out=memory[:], in_=mem)
         nc.sync.dma_start(slot_sb[:], slot)
+        load_weights(1, w2_words, w2_scales)
 
         warm = sb.tile([P, 2], F32, name="warm")
         nc.vector.memset(warm[:, 0:1], 0.0)
         nc.scalar.activation(out=warm[:, 1:2], in_=warm[:, 0:1], func=ACT.Sigmoid)
-
-        w_scales = sb.tile([P, 2 * N], U8, name="w_scales", align_bytes=64)
-        nc.gpsimd.memset(w_scales[:].bitcast(I32), 0)
-        for i, scales in enumerate((w1_scales, w2_scales)):
-            for q in range(4):
-                nc.gpsimd.dma_start(
-                    out=w_scales[32 * q : 32 * q + 4, i * N : (i + 1) * N].bitcast(I32),
-                    in_=scales[0, 4 * q : 4 * q + 4, :].bitcast(I32),
-                )
 
         pairs = [sb.tile([P, T, 2], BF16, name="pairs%d" % u) for u in range(2)]
         windows = [pairs[u][:].rearrange("p t e -> p (t e)").bitcast(U32) for u in range(2)]

@@ -19,14 +19,8 @@ ALU = mybir.AluOpType
 P = 128
 CH = 256
 NCH = S // CH
-LOADS = (
-    ((0, 1, 0, 2048), (1, 1, 0, 1280), (1, 1, 1280, 2048)),
-    ((0, 2, 0, 1024), (0, 1, 1024, 2048), (1, 1, 1024, 1664), (1, 1, 1664, 2048)),
-)
-CASTS = (
-    ((0, 800, 1280), (1280, 1760, 2048)),
-    ((0, 512, 1024), (1024, 1424, 1664), (1664, 1904, 2048)),
-)
+SPLIT = 384
+PIECES = ((0, 1280, 2048), (0, 1280, 2048), (0, 1280, 2048), (0, 1024, 1664, 2048))
 
 
 def tile_picked_gmem_tanh_e_kernel(tc, xT, mem, w1_words, w1_scales, w2_words, w2_scales, offs, slot, out):
@@ -40,11 +34,11 @@ def tile_picked_gmem_tanh_e_kernel(tc, xT, mem, w1_words, w1_scales, w2_words, w
         memory = sb.tile([P, U], F32, name="memory")
         x_rows = xT.rearrange("(p j) t -> p j t", j=4)
 
-        raw = [sb.tile([P, 2, T], F32, name="raw%d" % u) for u in range(2)]
-        for u in range(2):
-            for e, n, a, b in LOADS[u]:
-                nc.sync.dma_start(out=raw[u][:, e : e + n, a:b], in_=x_rows[:, 2 * u + e : 2 * u + e + n, a:b])
-            if u == 0:
+        raw = [sb.tile([P, T], F32, name="raw%d" % t) for t in range(4)]
+        for t in range(4):
+            for a, b in zip(PIECES[t], PIECES[t][1:]):
+                nc.sync.dma_start(out=raw[t][:, a:b], in_=x_rows[:, t, a:b])
+            if t == 0:
                 nc.sync.dma_start(offs_sb[:], offs)
         w_words = [sb.tile([P, 2 * N], U8, name="w_words%d" % i, align_bytes=64) for i in range(2)]
         w_scales = sb.tile([P, 2 * N], U8, name="w_scales", align_bytes=64)
@@ -67,36 +61,42 @@ def tile_picked_gmem_tanh_e_kernel(tc, xT, mem, w1_words, w1_scales, w2_words, w
         nc.vector.memset(warm[:, 0:1], 0.0)
         nc.scalar.activation(out=warm[:, 1:2], in_=warm[:, 0:1], func=ACT.Sigmoid)
 
-        pairs = [sb.tile([P, T, 2], BF16, name="pairs%d" % u) for u in range(2)]
-        windows = [pairs[u][:].rearrange("p t e -> p (t e)").bitcast(U32) for u in range(2)]
-
-        def cast(u):
-            for first, split, end in CASTS[u]:
-                for copy, a, b in ((nc.vector.tensor_copy, first, split), (nc.scalar.copy, split, end)):
-                    copy(out=pairs[u][:, a:b, :], in_=raw[u][:, :, a:b].rearrange("p e t -> p t e"))
-
         def entries(lst, a, b):
             return lst[:, a // 16 : b // 16]
 
-        grouped = [sb.tile([P, CH, 2], U32, name="grouped%d" % c, align_bytes=64) for c in range(NCH)]
-        halves = [sb.tile([P, 2, CH], U32, name="halves%d" % c) for c in range(NCH)]
+        rounded = [sb.tile([P, T], BF16, name="rounded%d" % t) for t in range(4)]
+        grouped = sb.tile([P, S * 4], BF16, name="grouped", align_bytes=64)
+        halves = sb.tile([P, 2, SPLIT], I32, name="halves")
 
-        def gather(u, c):
-            dst = halves[c][:, u, :]
-            nc.vector.tensor_copy(out=dst, in_=windows[u].indirect(entries(offs_sb, c * CH, (c + 1) * CH)))
+        def cast(t):
+            for a, b in zip(PIECES[t], PIECES[t][1:]):
+                nc.vector.tensor_copy(out=rounded[t][:, a:b], in_=raw[t][:, a:b])
 
-        cast(0)
-        for c in range(NCH):
-            gather(0, c)
-        cast(1)
+        def gather_vector(t):
+            dst = halves[:, t // 2, :].bitcast(BF16).rearrange("p (n e) -> p n e", e=2)[:, :, t % 2]
+            nc.vector.tensor_copy(out=dst, in_=raw[t][:].indirect(entries(offs_sb, 0, SPLIT)))
+
+        def gather_scalar(t, a, b):
+            dst = grouped[:, 4 * a : 4 * b].rearrange("p (n t) -> p n t", t=4)[:, :, t]
+            nc.scalar.activation(out=dst, in_=rounded[t][:].indirect(entries(offs_sb, a, b)), func=ACT.Copy)
+
+        for t in range(4):
+            cast(t)
+            gather_vector(t)
+            if t < 3:
+                gather_scalar(t, SPLIT, S)
+            else:
+                gather_scalar(t, SPLIT, S - CH)
+                gather_scalar(t, S - CH, S)
+        nc.vector.tensor_copy(
+            out=grouped[:, : 4 * SPLIT].bitcast(I32).rearrange("p (n u) -> p n u", u=2),
+            in_=halves[:].rearrange("p u n -> p n u"),
+        )
 
         cand = sb.tile([P, S], F32, name="cand")
         keep = sb.tile([P, S], F32, name="keep")
         diff = sb.tile([P, S], F32, name="diff")
         step = sb.tile([P, S], F32, name="step")
-
-        def weave(c):
-            nc.scalar.copy(out=grouped[c][:], in_=halves[c][:].rearrange("p u n -> p n u"))
 
         codes = sb.tile([P, S], U32, name="codes", align_bytes=64)
         scales = sb.tile([P, S], U8, name="scales", align_bytes=64)
@@ -105,7 +105,7 @@ def tile_picked_gmem_tanh_e_kernel(tc, xT, mem, w1_words, w1_scales, w2_words, w
             nc.vector.quantize_mx(
                 out=codes[:, c * CH : (c + 1) * CH].bitcast(FP8X4),
                 scales=scales[:, c * CH : (c + 1) * CH],
-                in_=grouped[c][:].rearrange("p n u -> p (n u)").bitcast(BF16),
+                in_=grouped[:, 4 * c * CH : 4 * (c + 1) * CH],
             )
 
         def product(i, a, b, dst, func, scale):
@@ -131,9 +131,6 @@ def tile_picked_gmem_tanh_e_kernel(tc, xT, mem, w1_words, w1_scales, w2_words, w
         def scatter(a, b):
             nc.vector.tensor_tensor(memory[:].indirect(entries(slot_sb, a, b)), step[:, a:b], cand[:, a:b], ALU.add)
 
-        for c in range(NCH):
-            gather(1, c)
-            weave(c)
         for c in range(NCH):
             quantise(c)
         for c in range(NCH):

@@ -20,6 +20,7 @@ P = 128
 CH = 256
 NCH = S // CH
 SPLIT = 384
+PARTS = ((0, SPLIT), (SPLIT, S - CH), (S - CH, S))
 PIECES = ((0, 1280, 2048), (0, 1280, 2048), (0, 1280, 2048), (0, 1024, 1664, 2048))
 
 
@@ -65,8 +66,8 @@ def tile_picked_gmem_tanh_e_kernel(tc, xT, mem, w1_words, w1_scales, w2_words, w
             return lst[:, a // 16 : b // 16]
 
         rounded = [sb.tile([P, T], BF16, name="rounded%d" % t) for t in range(4)]
-        grouped = sb.tile([P, S * 4], BF16, name="grouped", align_bytes=64)
-        halves = sb.tile([P, 2, SPLIT], I32, name="halves")
+        grouped = {a: sb.tile([P, 4 * (b - a)], BF16, name="grouped%d" % a, align_bytes=64) for a, b in PARTS}
+        halves = sb.tile([P, 2, SPLIT], I32, name="halves", tag="halves", align_bytes=64)
 
         def cast(t):
             for a, b in zip(PIECES[t], PIECES[t][1:]):
@@ -77,19 +78,16 @@ def tile_picked_gmem_tanh_e_kernel(tc, xT, mem, w1_words, w1_scales, w2_words, w
             nc.vector.tensor_copy(out=dst, in_=raw[t][:].indirect(entries(offs_sb, 0, SPLIT)))
 
         def gather_scalar(t, a, b):
-            dst = grouped[:, 4 * a : 4 * b].rearrange("p (n t) -> p n t", t=4)[:, :, t]
+            dst = grouped[a][:].rearrange("p (n t) -> p n t", t=4)[:, :, t]
             nc.scalar.activation(out=dst, in_=rounded[t][:].indirect(entries(offs_sb, a, b)), func=ACT.Copy)
 
         for t in range(4):
             cast(t)
             gather_vector(t)
-            if t < 3:
-                gather_scalar(t, SPLIT, S)
-            else:
-                gather_scalar(t, SPLIT, S - CH)
-                gather_scalar(t, S - CH, S)
+            for a, b in PARTS[1:]:
+                gather_scalar(t, a, b)
         nc.vector.tensor_copy(
-            out=grouped[:, : 4 * SPLIT].bitcast(I32).rearrange("p (n u) -> p n u", u=2),
+            out=grouped[0][:].bitcast(I32).rearrange("p (n u) -> p n u", u=2),
             in_=halves[:].rearrange("p u n -> p n u"),
         )
 
@@ -98,27 +96,34 @@ def tile_picked_gmem_tanh_e_kernel(tc, xT, mem, w1_words, w1_scales, w2_words, w
         diff = sb.tile([P, S], F32, name="diff")
         step = sb.tile([P, S], F32, name="step")
 
-        codes = sb.tile([P, S], U32, name="codes", align_bytes=64)
+        codes_vector = sb.tile([P, SPLIT], U32, name="codes_vector", align_bytes=64)
+        codes_scalar = sb.tile([P, S - SPLIT], U32, name="codes_scalar", tag="halves", align_bytes=64)
+
+        def codes(a, b):
+            return (codes_vector[:, a:b] if b <= SPLIT else codes_scalar[:, a - SPLIT : b - SPLIT]).bitcast(FP8X4)
+
         scales = sb.tile([P, S], U8, name="scales", align_bytes=64)
 
-        def quantise(c):
+        def quantise(first, a, b):
             nc.vector.quantize_mx(
-                out=codes[:, c * CH : (c + 1) * CH].bitcast(FP8X4),
-                scales=scales[:, c * CH : (c + 1) * CH],
-                in_=grouped[:, 4 * c * CH : 4 * (c + 1) * CH],
+                out=codes(a, b),
+                scales=scales[:, a:b],
+                in_=grouped[first][:, 4 * (a - first) : 4 * (b - first)],
             )
 
         def product(i, a, b, dst, func, scale):
             acc = ps.tile([P, b - a], F32, name="acc%d_%d" % (i, a))
-            nc.tensor.matmul_mx(
-                out=acc[:],
-                lhsT=w_words[i][:].bitcast(FP4X4),
-                lhsT_scale=w_scales[:, i * N : (i + 1) * N],
-                rhs=codes[:, a:b].bitcast(FP8X4),
-                rhs_scale=scales[:, a:b],
-                start=True,
-                stop=True,
-            )
+            cuts = (a, CH, SPLIT, b) if a < CH < SPLIT < b else (a, SPLIT, b) if a < SPLIT < b else (a, b)
+            for lo, hi in zip(cuts, cuts[1:]):
+                nc.tensor.matmul_mx(
+                    out=acc[:, lo - a : hi - a],
+                    lhsT=w_words[i][:].bitcast(FP4X4),
+                    lhsT_scale=w_scales[:, i * N : (i + 1) * N],
+                    rhs=codes(lo, hi),
+                    rhs_scale=scales[:, lo:hi],
+                    start=True,
+                    stop=True,
+                )
             nc.scalar.activation(out=dst[:, a:b], in_=acc[:], func=func, scale=scale)
 
         def subtract(c):
@@ -131,8 +136,9 @@ def tile_picked_gmem_tanh_e_kernel(tc, xT, mem, w1_words, w1_scales, w2_words, w
         def scatter(a, b):
             nc.vector.tensor_tensor(memory[:].indirect(entries(slot_sb, a, b)), step[:, a:b], cand[:, a:b], ALU.add)
 
-        for c in range(NCH):
-            quantise(c)
+        for first, end in PARTS:
+            for a in range(first, end, CH):
+                quantise(first, a, min(a + CH, end))
         for c in range(NCH):
             product(0, c * CH, (c + 1) * CH, cand, ACT.Tanh, 1.0)
         for a in (0, 512):

@@ -17,11 +17,11 @@ ACT = mybir.ActivationFunctionType
 ALU = mybir.AluOpType
 
 P = 128
-CH = 256
-NCH = S // CH
-SPLIT = 384
-PARTS = ((0, SPLIT), (SPLIT, S - CH), (S - CH, S))
+GROUPS = ((0, 256), (768, 1024), (256, 512), (512, 768))
+STEPS = ((0, 128), (128, 256)) + GROUPS[1:]
+V0, V1 = 640, 1024
 PIECES = ((0, 1280, 2048), (0, 1280, 2048), (0, 1280, 2048), (0, 1024, 1664, 2048))
+MULTS = (0, 512, 1024)
 
 
 def tile_picked_gmem_tanh_e_kernel(tc, xT, mem, w1_words, w1_scales, w2_words, w2_scales, offs, slot, out):
@@ -34,6 +34,19 @@ def tile_picked_gmem_tanh_e_kernel(tc, xT, mem, w1_words, w1_scales, w2_words, w
         slot_sb = sb.tile([P, S // 16], U16, name="slot_sb")
         memory = sb.tile([P, U], F32, name="memory")
         x_rows = xT.rearrange("(p j) t -> p j t", j=4)
+        w_words = [sb.tile([P, 2 * N], U8, name="w_words%d" % i, align_bytes=64) for i in range(2)]
+        w_scales = sb.tile([P, 2 * N], U8, name="w_scales", align_bytes=64)
+        nc.gpsimd.memset(w_scales[:].bitcast(I32), 0)
+
+        def load_words(i, words):
+            nc.sync.dma_start(out=w_words[i][:].bitcast(I32), in_=words[0].bitcast(I32))
+
+        def load_scales(i, scales):
+            for q in range(4):
+                nc.sync.dma_start(
+                    out=w_scales[32 * q : 32 * q + 4, i * N : (i + 1) * N].bitcast(I32),
+                    in_=scales[0, 4 * q : 4 * q + 4, :].bitcast(I32),
+                )
 
         raw = [sb.tile([P, T], F32, name="raw%d" % t) for t in range(4)]
         for t in range(4):
@@ -41,22 +54,12 @@ def tile_picked_gmem_tanh_e_kernel(tc, xT, mem, w1_words, w1_scales, w2_words, w
                 nc.sync.dma_start(out=raw[t][:, a:b], in_=x_rows[:, t, a:b])
             if t == 0:
                 nc.sync.dma_start(offs_sb[:], offs)
-        w_words = [sb.tile([P, 2 * N], U8, name="w_words%d" % i, align_bytes=64) for i in range(2)]
-        w_scales = sb.tile([P, 2 * N], U8, name="w_scales", align_bytes=64)
-        nc.vector.memset(w_scales[:].bitcast(I32), 0)
-
-        def load_weights(i, words, scales):
-            nc.sync.dma_start(out=w_words[i][:].bitcast(I32), in_=words[0].bitcast(I32))
-            for q in range(4):
-                nc.sync.dma_start(
-                    out=w_scales[32 * q : 32 * q + 4, i * N : (i + 1) * N].bitcast(I32),
-                    in_=scales[0, 4 * q : 4 * q + 4, :].bitcast(I32),
-                )
-
-        load_weights(0, w1_words, w1_scales)
+        load_words(0, w1_words)
+        load_scales(0, w1_scales)
         nc.sync.dma_start(out=memory[:], in_=mem)
         nc.sync.dma_start(slot_sb[:], slot)
-        load_weights(1, w2_words, w2_scales)
+        load_words(1, w2_words)
+        load_scales(1, w2_scales)
 
         warm = sb.tile([P, 2], F32, name="warm")
         nc.vector.memset(warm[:, 0:1], 0.0)
@@ -66,55 +69,67 @@ def tile_picked_gmem_tanh_e_kernel(tc, xT, mem, w1_words, w1_scales, w2_words, w
             return lst[:, a // 16 : b // 16]
 
         rounded = [sb.tile([P, T], BF16, name="rounded%d" % t) for t in range(4)]
-        grouped = {a: sb.tile([P, 4 * (b - a)], BF16, name="grouped%d" % a, align_bytes=64) for a, b in PARTS}
-        halves = sb.tile([P, 2, SPLIT], I32, name="halves", tag="halves", align_bytes=64)
+        grouped_head = sb.tile([P, 4 * 768], BF16, name="grouped_head", align_bytes=64)
+        grouped_tail = sb.tile([P, 4 * 256], BF16, name="grouped_tail", align_bytes=64)
+        halves = sb.tile([P, 2, V1 - V0], I32, name="halves", tag="halves", align_bytes=64)
+
+        def group_view(a, b):
+            return grouped_head[:, 4 * a : 4 * b] if b <= 768 else grouped_tail[:, 4 * (a - 768) : 4 * (b - 768)]
 
         def cast(t):
             for a, b in zip(PIECES[t], PIECES[t][1:]):
+                if t == 0 and b == T:
+                    nc.scalar.activation(out=rounded[t][:, b - 256 : b], in_=raw[t][:, b - 256 : b], func=ACT.Copy)
+                    b = b - 256
                 nc.vector.tensor_copy(out=rounded[t][:, a:b], in_=raw[t][:, a:b])
 
-        def gather_vector(t):
-            dst = halves[:, t // 2, :].bitcast(BF16).rearrange("p (n e) -> p n e", e=2)[:, :, t % 2]
-            nc.vector.tensor_copy(out=dst, in_=raw[t][:].indirect(entries(offs_sb, 0, SPLIT)))
+        def gather_vector(t, a, b):
+            dst = halves[:, t // 2, a - V0 : b - V0].bitcast(BF16).rearrange("p (n e) -> p n e", e=2)[:, :, t % 2]
+            nc.vector.tensor_copy(out=dst, in_=raw[t][:].indirect(entries(offs_sb, a, b)))
 
         def gather_scalar(t, a, b):
-            dst = grouped[a][:].rearrange("p (n t) -> p n t", t=4)[:, :, t]
+            dst = group_view(a, b).rearrange("p (n t) -> p n t", t=4)[:, :, t]
             nc.scalar.activation(out=dst, in_=rounded[t][:].indirect(entries(offs_sb, a, b)), func=ACT.Copy)
+
+        def weave(a, b):
+            nc.vector.tensor_copy(
+                out=group_view(a, b).bitcast(I32).rearrange("p (n u) -> p n u", u=2),
+                in_=halves[:, :, a - V0 : b - V0].rearrange("p u n -> p n u"),
+            )
+
+        codes_outer = sb.tile([P, 512], U32, name="codes_outer", align_bytes=64)
+        codes_inner = sb.tile([P, 512], U32, name="codes_inner", tag="halves", align_bytes=64)
+
+        def codes(a, b):
+            if 256 <= a < 768:
+                return codes_inner[:, a - 256 : b - 256].bitcast(FP8X4)
+            return (codes_outer[:, a:b] if a < 256 else codes_outer[:, a - 512 : b - 512]).bitcast(FP8X4)
+
+        scales = sb.tile([P, S], U8, name="scales", align_bytes=64)
+
+        def quantise(g):
+            a, b = GROUPS[g]
+            nc.vector.quantize_mx(out=codes(a, b), scales=scales[:, a:b], in_=group_view(a, b))
 
         for t in range(4):
             cast(t)
-            gather_vector(t)
-            for a, b in PARTS[1:]:
+            gather_vector(t, V0, V1)
+            for a, b in ((0, V0),) if t < 3 else ((0, 256), (256, V0)):
                 gather_scalar(t, a, b)
-        nc.vector.tensor_copy(
-            out=grouped[0][:].bitcast(I32).rearrange("p (n u) -> p n u", u=2),
-            in_=halves[:].rearrange("p u n -> p n u"),
-        )
+        quantise(0)
+        weave(768, V1)
+        weave(V0, 768)
+        for g in range(1, 4):
+            quantise(g)
 
         cand = sb.tile([P, S], F32, name="cand")
         keep = sb.tile([P, S], F32, name="keep")
         diff = sb.tile([P, S], F32, name="diff")
         step = sb.tile([P, S], F32, name="step")
 
-        codes_vector = sb.tile([P, SPLIT], U32, name="codes_vector", align_bytes=64)
-        codes_scalar = sb.tile([P, S - SPLIT], U32, name="codes_scalar", tag="halves", align_bytes=64)
-
-        def codes(a, b):
-            return (codes_vector[:, a:b] if b <= SPLIT else codes_scalar[:, a - SPLIT : b - SPLIT]).bitcast(FP8X4)
-
-        scales = sb.tile([P, S], U8, name="scales", align_bytes=64)
-
-        def quantise(first, a, b):
-            nc.vector.quantize_mx(
-                out=codes(a, b),
-                scales=scales[:, a:b],
-                in_=grouped[first][:, 4 * (a - first) : 4 * (b - first)],
-            )
-
         def product(i, a, b, dst, func, scale):
             acc = ps.tile([P, b - a], F32, name="acc%d_%d" % (i, a))
-            cuts = (a, CH, SPLIT, b) if a < CH < SPLIT < b else (a, SPLIT, b) if a < SPLIT < b else (a, b)
-            for lo, hi in zip(cuts, cuts[1:]):
+            for lo, hi in ((a, a + 256), (a + 256, b)) if b - a > 256 else ((a, b),):
                 nc.tensor.matmul_mx(
                     out=acc[:, lo - a : hi - a],
                     lhsT=w_words[i][:].bitcast(FP4X4),
@@ -126,26 +141,13 @@ def tile_picked_gmem_tanh_e_kernel(tc, xT, mem, w1_words, w1_scales, w2_words, w
                 )
             nc.scalar.activation(out=dst[:, a:b], in_=acc[:], func=func, scale=scale)
 
-        def subtract(c):
-            cols = slice(c * CH, (c + 1) * CH)
-            nc.vector.tensor_tensor(diff[:, cols], memory[:].indirect(entries(slot_sb, cols.start, cols.stop)), cand[:, cols], ALU.subtract)
-
-        def scale_diff(a, b):
-            nc.vector.tensor_tensor(step[:, a:b], diff[:, a:b], keep[:, a:b], ALU.mult)
-
-        def scatter(a, b):
-            nc.vector.tensor_tensor(memory[:].indirect(entries(slot_sb, a, b)), step[:, a:b], cand[:, a:b], ALU.add)
-
-        for first, end in PARTS:
-            for a in range(first, end, CH):
-                quantise(first, a, min(a + CH, end))
-        for c in range(NCH):
-            product(0, c * CH, (c + 1) * CH, cand, ACT.Tanh, 1.0)
+        for a, b in STEPS:
+            product(0, a, b, cand, ACT.Tanh, 1.0)
         for a in (0, 512):
             product(1, a, a + 512, keep, ACT.Sigmoid, -1.0)
-        for c in range(NCH):
-            subtract(c)
-        scale_diff(0, 512)
-        scale_diff(512, 1024)
-        scatter(0, 1024)
+        for a, b in STEPS:
+            nc.vector.tensor_tensor(diff[:, a:b], memory[:].indirect(entries(slot_sb, a, b)), cand[:, a:b], ALU.subtract)
+        for a, b in zip(MULTS, MULTS[1:]):
+            nc.vector.tensor_tensor(step[:, a:b], diff[:, a:b], keep[:, a:b], ALU.mult)
+        nc.vector.tensor_tensor(memory[:].indirect(slot_sb[:]), step[:], cand[:], ALU.add)
         nc.sync.dma_start(out=out, in_=memory[:])

@@ -17,10 +17,10 @@ ACT = mybir.ActivationFunctionType
 ALU = mybir.AluOpType
 
 P = 128
-GROUPS = ((0, 256), (768, 1024), (256, 512), (512, 768))
+GROUPS = ((0, 256), (256, 512), (512, 768), (768, 1024))
 STEPS = ((0, 128), (128, 256)) + GROUPS[1:]
-V0, V1 = 640, 1024
-PIECES = ((0, 1280, 2048), (0, 1280, 2048), (0, 1280, 2048), (0, 1024, 1664, 2048))
+SPLIT = 352
+PIECES = ((0, 1280, 2048), (0, 1280, 2048), (0, 1280, 2048), (0, 1408, 2048))
 MULTS = (0, 512, 1024)
 
 
@@ -69,12 +69,10 @@ def tile_picked_gmem_tanh_e_kernel(tc, xT, mem, w1_words, w1_scales, w2_words, w
             return lst[:, a // 16 : b // 16]
 
         rounded = [sb.tile([P, T], BF16, name="rounded%d" % t) for t in range(4)]
-        grouped_head = sb.tile([P, 4 * 768], BF16, name="grouped_head", align_bytes=64)
-        grouped_tail = sb.tile([P, 4 * 256], BF16, name="grouped_tail", align_bytes=64)
-        halves = sb.tile([P, 2, V1 - V0], I32, name="halves", tag="halves", align_bytes=64)
+        grouped = sb.tile([P, 4 * S], BF16, name="grouped", align_bytes=64)
 
         def group_view(a, b):
-            return grouped_head[:, 4 * a : 4 * b] if b <= 768 else grouped_tail[:, 4 * (a - 768) : 4 * (b - 768)]
+            return grouped[:, 4 * a : 4 * b]
 
         def cast(t):
             for a, b in zip(PIECES[t], PIECES[t][1:]):
@@ -84,26 +82,17 @@ def tile_picked_gmem_tanh_e_kernel(tc, xT, mem, w1_words, w1_scales, w2_words, w
                 nc.vector.tensor_copy(out=rounded[t][:, a:b], in_=raw[t][:, a:b])
 
         def gather_vector(t, a, b):
-            dst = halves[:, t // 2, a - V0 : b - V0].bitcast(BF16).rearrange("p (n e) -> p n e", e=2)[:, :, t % 2]
+            dst = group_view(a, b).rearrange("p (n t) -> p n t", t=4)[:, :, t]
             nc.vector.tensor_copy(out=dst, in_=raw[t][:].indirect(entries(offs_sb, a, b)))
 
         def gather_scalar(t, a, b):
             dst = group_view(a, b).rearrange("p (n t) -> p n t", t=4)[:, :, t]
             nc.scalar.activation(out=dst, in_=rounded[t][:].indirect(entries(offs_sb, a, b)), func=ACT.Copy)
 
-        def weave(a, b):
-            nc.vector.tensor_copy(
-                out=group_view(a, b).bitcast(I32).rearrange("p (n u) -> p n u", u=2),
-                in_=halves[:, :, a - V0 : b - V0].rearrange("p u n -> p n u"),
-            )
-
-        codes_outer = sb.tile([P, 512], U32, name="codes_outer", align_bytes=64)
-        codes_inner = sb.tile([P, 512], U32, name="codes_inner", tag="halves", align_bytes=64)
+        codes_sb = sb.tile([P, S], U32, name="codes_sb", align_bytes=64)
 
         def codes(a, b):
-            if 256 <= a < 768:
-                return codes_inner[:, a - 256 : b - 256].bitcast(FP8X4)
-            return (codes_outer[:, a:b] if a < 256 else codes_outer[:, a - 512 : b - 512]).bitcast(FP8X4)
+            return codes_sb[:, a:b].bitcast(FP8X4)
 
         scales = sb.tile([P, S], U8, name="scales", align_bytes=64)
 
@@ -113,13 +102,10 @@ def tile_picked_gmem_tanh_e_kernel(tc, xT, mem, w1_words, w1_scales, w2_words, w
 
         for t in range(4):
             cast(t)
-            gather_vector(t, V0, V1)
-            for a, b in ((0, V0),) if t < 3 else ((0, 256), (256, V0)):
+            gather_vector(t, 0, SPLIT)
+            for a, b in ((SPLIT, S),) if t < 3 else ((SPLIT, 768), (768, S)):
                 gather_scalar(t, a, b)
-        quantise(0)
-        weave(768, V1)
-        weave(V0, 768)
-        for g in range(1, 4):
+        for g in range(4):
             quantise(g)
 
         cand = sb.tile([P, S], F32, name="cand")
@@ -129,7 +115,7 @@ def tile_picked_gmem_tanh_e_kernel(tc, xT, mem, w1_words, w1_scales, w2_words, w
 
         def product(i, a, b, dst, func, scale):
             acc = ps.tile([P, b - a], F32, name="acc%d_%d" % (i, a))
-            for lo, hi in ((a, a + 256), (a + 256, b)) if b - a > 256 else ((a, b),):
+            for lo, hi in ((a, b),):
                 nc.tensor.matmul_mx(
                     out=acc[:, lo - a : hi - a],
                     lhsT=w_words[i][:].bitcast(FP4X4),

@@ -21,7 +21,7 @@ GROUPS = ((0, 256), (256, 512), (512, 768), (768, 1024))
 STEPS = ((0, 128), (128, 256)) + GROUPS[1:]
 SPLIT = 352
 PIECES = ((0, 1280, 2048), (0, 1280, 2048), (0, 1280, 2048), (0, 1408, 2048))
-MULTS = (0, 512, 1024)
+FIRST = 256
 
 
 def tile_picked_gmem_tanh_e_kernel(tc, xT, mem, w1_words, w1_scales, w2_words, w2_scales, offs, slot, out):
@@ -127,13 +127,21 @@ def tile_picked_gmem_tanh_e_kernel(tc, xT, mem, w1_words, w1_scales, w2_words, w
                 )
             nc.scalar.activation(out=dst[:, a:b], in_=acc[:], func=func, scale=scale)
 
+        fresh = sb.tile([P, FIRST], F32, name="fresh")
+
+        def diff_at(a, b):
+            return step[:, a + 256 : b + 256] if a == 256 else diff[:, a:b]
+
         for a, b in STEPS:
             product(0, a, b, cand, ACT.Tanh, 1.0)
-        for a in (0, 512):
-            product(1, a, a + 512, keep, ACT.Sigmoid, -1.0)
+        for a, b in ((0, 256), (256, 512), (512, S)):
+            product(1, a, b, keep, ACT.Sigmoid, -1.0)
         for a, b in STEPS:
-            nc.vector.tensor_tensor(diff[:, a:b], memory[:].indirect(entries(slot_sb, a, b)), cand[:, a:b], ALU.subtract)
-        for a, b in zip(MULTS, MULTS[1:]):
-            nc.vector.tensor_tensor(step[:, a:b], diff[:, a:b], keep[:, a:b], ALU.mult)
-        nc.vector.tensor_tensor(memory[:].indirect(slot_sb[:]), step[:], cand[:], ALU.add)
+            nc.vector.tensor_tensor(diff_at(a, b), memory[:].indirect(entries(slot_sb, a, b)), cand[:, a:b], ALU.subtract)
+        nc.vector.tensor_tensor(step[:, 0:FIRST], diff[:, 0:FIRST], keep[:, 0:FIRST], ALU.mult)
+        nc.vector.tensor_tensor(step[:, FIRST:512], diff_at(FIRST, 512), keep[:, FIRST:512], ALU.mult)
+        nc.vector.tensor_tensor(fresh[:], step[:, 0:FIRST], cand[:, 0:FIRST], ALU.add)
+        nc.vector.tensor_copy(out=memory[:].indirect(entries(slot_sb, 0, FIRST)), in_=fresh[:])
+        nc.gpsimd.tensor_tensor(step[:, 512:S], diff[:, 512:S], keep[:, 512:S], ALU.mult)
+        nc.vector.tensor_tensor(memory[:].indirect(entries(slot_sb, FIRST, S)), step[:, FIRST:S], cand[:, FIRST:S], ALU.add)
         nc.sync.dma_start(out=out, in_=memory[:])

@@ -21,6 +21,7 @@ GROUPS = ((0, 256), (256, 512), (512, 768), (768, 1024))
 STEPS = ((0, 128), (128, 256)) + GROUPS[1:]
 SPLIT = 352
 PIECES = ((0, 1280, 2048), (0, 1280, 2048), (0, 1280, 2048), (0, 1408, 2048))
+POOL = 384
 FIRST = 256
 
 
@@ -60,6 +61,8 @@ def tile_picked_gmem_tanh_e_kernel(tc, xT, mem, w1_words, w1_scales, w2_words, w
         nc.sync.dma_start(slot_sb[:], slot)
         load_words(1, w2_words)
         load_scales(1, w2_scales)
+        result = sb.tile([P, U], F32, name="result")
+        nc.sync.dma_start(out=result[:], in_=mem)
 
         warm = sb.tile([P, 2], F32, name="warm")
         nc.vector.memset(warm[:, 0:1], 0.0)
@@ -113,35 +116,54 @@ def tile_picked_gmem_tanh_e_kernel(tc, xT, mem, w1_words, w1_scales, w2_words, w
         diff = sb.tile([P, S], F32, name="diff")
         step = sb.tile([P, S], F32, name="step")
 
-        def product(i, a, b, dst, func, scale):
-            acc = ps.tile([P, b - a], F32, name="acc%d_%d" % (i, a))
-            for lo, hi in ((a, b),):
-                nc.tensor.matmul_mx(
-                    out=acc[:, lo - a : hi - a],
-                    lhsT=w_words[i][:].bitcast(FP4X4),
-                    lhsT_scale=w_scales[:, i * N : (i + 1) * N],
-                    rhs=codes(lo, hi),
-                    rhs_scale=scales[:, lo:hi],
-                    start=True,
-                    stop=True,
-                )
-            nc.scalar.activation(out=dst[:, a:b], in_=acc[:], func=func, scale=scale)
+        def multiply(acc, i, a, b):
+            nc.tensor.matmul_mx(
+                out=acc,
+                lhsT=w_words[i][:].bitcast(FP4X4),
+                lhsT_scale=w_scales[:, i * N : (i + 1) * N],
+                rhs=codes(a, b),
+                rhs_scale=scales[:, a:b],
+                start=True,
+                stop=True,
+            )
+
+        def candidate(acc, a, b):
+            nc.scalar.activation(out=cand[:, a:b], in_=acc, func=ACT.Tanh)
+
+        def gate(acc, a, b):
+            nc.scalar.activation(out=keep[:, a:b], in_=acc, func=ACT.Sigmoid, scale=-1.0)
+
+        for a, b in STEPS[:4]:
+            acc = ps.tile([P, b - a], F32, name="acc0_%d" % a)
+            multiply(acc[:], 0, a, b)
+            candidate(acc[:], a, b)
+        shared = ps.tile([P, 512], F32, name="shared")
+        multiply(shared[:, 256:512], 0, 768, S)
+        multiply(shared[:, 0:256], 1, 0, 256)
+        second = ps.tile([P, 256], F32, name="second")
+        multiply(second[:], 1, 256, 512)
+        third = ps.tile([P, 512], F32, name="third")
+        multiply(third[:], 1, 512, S)
+        gate(shared[:, 0:256], 0, 256)
+        candidate(shared[:, 256:384], 768, 896)
+        gate(second[:, 0:128], 256, 384)
+        candidate(shared[:, 384:512], 896, S)
+        gate(second[:, 128:256], 384, 512)
+        gate(third[:], 512, S)
 
         fresh = sb.tile([P, FIRST], F32, name="fresh")
 
-        def diff_at(a, b):
-            return step[:, a + 256 : b + 256] if a == 256 else diff[:, a:b]
+        def subtract(a, b):
+            nc.vector.tensor_tensor(diff[:, a:b], memory[:].indirect(entries(slot_sb, a, b)), cand[:, a:b], ALU.subtract)
 
-        for a, b in STEPS:
-            product(0, a, b, cand, ACT.Tanh, 1.0)
-        for a, b in ((0, 256), (256, 512), (512, S)):
-            product(1, a, b, keep, ACT.Sigmoid, -1.0)
-        for a, b in STEPS:
-            nc.vector.tensor_tensor(diff_at(a, b), memory[:].indirect(entries(slot_sb, a, b)), cand[:, a:b], ALU.subtract)
+        for a, b in STEPS[:4]:
+            subtract(a, b)
         nc.vector.tensor_tensor(step[:, 0:FIRST], diff[:, 0:FIRST], keep[:, 0:FIRST], ALU.mult)
-        nc.vector.tensor_tensor(step[:, FIRST:512], diff_at(FIRST, 512), keep[:, FIRST:512], ALU.mult)
+        subtract(768, 896)
+        nc.vector.tensor_tensor(step[:, FIRST:POOL], diff[:, FIRST:POOL], keep[:, FIRST:POOL], ALU.mult)
         nc.vector.tensor_tensor(fresh[:], step[:, 0:FIRST], cand[:, 0:FIRST], ALU.add)
-        nc.vector.tensor_copy(out=memory[:].indirect(entries(slot_sb, 0, FIRST)), in_=fresh[:])
-        nc.gpsimd.tensor_tensor(step[:, 512:S], diff[:, 512:S], keep[:, 512:S], ALU.mult)
-        nc.vector.tensor_tensor(memory[:].indirect(entries(slot_sb, FIRST, S)), step[:, FIRST:S], cand[:, FIRST:S], ALU.add)
-        nc.sync.dma_start(out=out, in_=memory[:])
+        subtract(896, S)
+        nc.vector.tensor_copy(out=result[:].indirect(entries(slot_sb, 0, FIRST)), in_=fresh[:])
+        nc.gpsimd.tensor_tensor(step[:, POOL:S], diff[:, POOL:S], keep[:, POOL:S], ALU.mult)
+        nc.vector.tensor_tensor(result[:].indirect(entries(slot_sb, FIRST, S)), step[:, FIRST:S], cand[:, FIRST:S], ALU.add)
+        nc.sync.dma_start(out=out, in_=result[:])

@@ -21,7 +21,7 @@ GROUPS = ((0, 256), (256, 512), (512, 768), (768, 1024))
 STEPS = ((0, 128), (128, 256)) + GROUPS[1:]
 SPLIT = 352
 PIECES = ((0, 1280, 2048), (0, 1280, 2048), (0, 1280, 2048), (0, 1408, 2048))
-POOL = 384
+POOL = 512
 FIRST = 256
 
 
@@ -61,8 +61,6 @@ def tile_picked_gmem_tanh_e_kernel(tc, xT, mem, w1_words, w1_scales, w2_words, w
         nc.sync.dma_start(slot_sb[:], slot)
         load_words(1, w2_words)
         load_scales(1, w2_scales)
-        result = sb.tile([P, U], F32, name="result")
-        nc.sync.dma_start(out=result[:], in_=mem)
 
         warm = sb.tile([P, 2], F32, name="warm")
         nc.vector.memset(warm[:, 0:1], 0.0)
@@ -145,10 +143,8 @@ def tile_picked_gmem_tanh_e_kernel(tc, xT, mem, w1_words, w1_scales, w2_words, w
         third = ps.tile([P, 512], F32, name="third")
         multiply(third[:], 1, 512, S)
         gate(shared[:, 0:256], 0, 256)
-        candidate(shared[:, 256:384], 768, 896)
-        gate(second[:, 0:128], 256, 384)
-        candidate(shared[:, 384:512], 896, S)
-        gate(second[:, 128:256], 384, 512)
+        candidate(shared[:, 256:512], 768, S)
+        gate(second[:], 256, 512)
         gate(third[:], 512, S)
 
         fresh = sb.tile([P, FIRST], F32, name="fresh")
@@ -158,12 +154,12 @@ def tile_picked_gmem_tanh_e_kernel(tc, xT, mem, w1_words, w1_scales, w2_words, w
 
         for a, b in STEPS[:4]:
             subtract(a, b)
-        nc.vector.tensor_tensor(step[:, 0:FIRST], diff[:, 0:FIRST], keep[:, 0:FIRST], ALU.mult)
-        subtract(768, 896)
+        early = step[:, POOL : POOL + FIRST]
+        nc.vector.tensor_tensor(early, diff[:, 0:FIRST], keep[:, 0:FIRST], ALU.mult)
+        subtract(768, S)
+        nc.vector.tensor_tensor(fresh[:], early, cand[:, 0:FIRST], ALU.add)
         nc.vector.tensor_tensor(step[:, FIRST:POOL], diff[:, FIRST:POOL], keep[:, FIRST:POOL], ALU.mult)
-        nc.vector.tensor_tensor(fresh[:], step[:, 0:FIRST], cand[:, 0:FIRST], ALU.add)
-        subtract(896, S)
-        nc.vector.tensor_copy(out=result[:].indirect(entries(slot_sb, 0, FIRST)), in_=fresh[:])
+        nc.vector.tensor_copy(out=memory[:].indirect(entries(slot_sb, 0, FIRST)), in_=fresh[:])
         nc.gpsimd.tensor_tensor(step[:, POOL:S], diff[:, POOL:S], keep[:, POOL:S], ALU.mult)
-        nc.vector.tensor_tensor(result[:].indirect(entries(slot_sb, FIRST, S)), step[:, FIRST:S], cand[:, FIRST:S], ALU.add)
-        nc.sync.dma_start(out=out, in_=result[:])
+        nc.vector.tensor_tensor(memory[:].indirect(entries(slot_sb, FIRST, S)), step[:, FIRST:S], cand[:, FIRST:S], ALU.add)
+        nc.sync.dma_start(out=out, in_=memory[:])

@@ -42,13 +42,14 @@ def tile_picked_gmem_tanh_e_kernel(tc, xT, mem, w1_words, w1_scales, w2_words, w
         def load_words(i, words):
             nc.sync.dma_start(out=w_words[i][:].bitcast(I32), in_=words[0].bitcast(I32))
 
-        def load_scales(i, scales):
+        def load_scales(i, scales, queue):
             for q in range(4):
-                nc.sync.dma_start(
+                queue.dma_start(
                     out=w_scales[32 * q : 32 * q + 4, i * N : (i + 1) * N].bitcast(I32),
                     in_=scales[0, 4 * q : 4 * q + 4, :].bitcast(I32),
                 )
 
+        load_scales(0, w1_scales, nc.scalar)
         raw = [sb.tile([P, T], F32, name="raw%d" % t) for t in range(4)]
         for t in range(4):
             for a, b in zip(PIECES[t], PIECES[t][1:]):
@@ -56,11 +57,10 @@ def tile_picked_gmem_tanh_e_kernel(tc, xT, mem, w1_words, w1_scales, w2_words, w
             if t == 0:
                 nc.sync.dma_start(offs_sb[:], offs)
         load_words(0, w1_words)
-        load_scales(0, w1_scales)
         nc.sync.dma_start(out=memory[:], in_=mem)
         nc.sync.dma_start(slot_sb[:], slot)
         load_words(1, w2_words)
-        load_scales(1, w2_scales)
+        load_scales(1, w2_scales, nc.sync)
 
         warm = sb.tile([P, 2], F32, name="warm")
         nc.vector.memset(warm[:, 0:1], 0.0)

@@ -19,8 +19,9 @@ ALU = mybir.AluOpType
 P = 128
 GROUPS = ((0, 256), (256, 512), (512, 768), (768, 1024))
 STEPS = ((0, 128), (128, 256)) + GROUPS[1:]
-SPLIT = 352
-PIECES = ((0, 1280, 2048), (0, 1280, 2048), (0, 1280, 2048), (0, 1408, 2048))
+PLANES = (0, 2, 1, 3)
+SPLITS = (352, 352, 288, 512)
+PIECES = ((0, 1280, 2048), (0, 1280, 2048), (0, 1280, 2048), (0, 1152, 1664, 2048))
 POOL = 512
 FIRST = 256
 
@@ -53,7 +54,7 @@ def tile_picked_gmem_tanh_e_kernel(tc, xT, mem, w1_words, w1_scales, w2_words, w
         raw = [sb.tile([P, T], F32, name="raw%d" % t) for t in range(4)]
         for t in range(4):
             for a, b in zip(PIECES[t], PIECES[t][1:]):
-                nc.sync.dma_start(out=raw[t][:, a:b], in_=x_rows[:, t, a:b])
+                nc.sync.dma_start(out=raw[t][:, a:b], in_=x_rows[:, PLANES[t], a:b])
             if t == 0:
                 nc.sync.dma_start(offs_sb[:], offs)
         load_words(0, w1_words)
@@ -69,7 +70,7 @@ def tile_picked_gmem_tanh_e_kernel(tc, xT, mem, w1_words, w1_scales, w2_words, w
         def entries(lst, a, b):
             return lst[:, a // 16 : b // 16]
 
-        rounded = [sb.tile([P, T], BF16, name="rounded%d" % t) for t in range(4)]
+        rounded = [sb.tile([P, T], BF16, name="rounded%d" % t) for t in range(2)] * 2
         grouped = sb.tile([P, 4 * S], BF16, name="grouped", align_bytes=64)
 
         def group_view(a, b):
@@ -83,11 +84,11 @@ def tile_picked_gmem_tanh_e_kernel(tc, xT, mem, w1_words, w1_scales, w2_words, w
                 nc.vector.tensor_copy(out=rounded[t][:, a:b], in_=raw[t][:, a:b])
 
         def gather_vector(t, a, b):
-            dst = group_view(a, b).rearrange("p (n t) -> p n t", t=4)[:, :, t]
+            dst = group_view(a, b).rearrange("p (n t) -> p n t", t=4)[:, :, PLANES[t]]
             nc.vector.tensor_copy(out=dst, in_=raw[t][:].indirect(entries(offs_sb, a, b)))
 
         def gather_scalar(t, a, b):
-            dst = group_view(a, b).rearrange("p (n t) -> p n t", t=4)[:, :, t]
+            dst = group_view(a, b).rearrange("p (n t) -> p n t", t=4)[:, :, PLANES[t]]
             nc.scalar.activation(out=dst, in_=rounded[t][:].indirect(entries(offs_sb, a, b)), func=ACT.Copy)
 
         codes_sb = sb.tile([P, S], U32, name="codes_sb", align_bytes=64)
@@ -103,9 +104,14 @@ def tile_picked_gmem_tanh_e_kernel(tc, xT, mem, w1_words, w1_scales, w2_words, w
 
         for t in range(4):
             cast(t)
-            gather_vector(t, 0, SPLIT)
-            for a, b in ((SPLIT, S),) if t < 3 else ((SPLIT, 768), (768, S)):
-                gather_scalar(t, a, b)
+            if t < 3:
+                gather_vector(t, 0, SPLITS[t])
+                gather_scalar(t, SPLITS[t], S)
+            else:
+                for a, b in GROUPS[:2]:
+                    gather_vector(t, a, b)
+                for a, b in GROUPS[2:]:
+                    gather_scalar(t, a, b)
         for g in range(4):
             quantise(g)
 

@@ -21,7 +21,7 @@ GROUPS = ((0, 256), (256, 512), (512, 768), (768, 1024))
 STEPS = ((0, 128), (128, 256)) + GROUPS[1:]
 PLANES = (0, 2, 1, 3)
 SPLITS = (352, 352, 288, 512)
-PIECES = ((0, 1280, 2048), (0, 1280, 2048), (0, 1280, 2048), (0, 1152, 1664, 2048))
+PIECES = ((0, 1280, 2048), (0, 1280, 2048), (0, 1280, 2048), (0, 1152, 1792, 2048))
 POOL = 512
 FIRST = 256
 
@@ -98,8 +98,7 @@ def tile_picked_gmem_tanh_e_kernel(tc, xT, mem, w1_words, w1_scales, w2_words, w
 
         scales = sb.tile([P, S], U8, name="scales", align_bytes=64)
 
-        def quantise(g):
-            a, b = GROUPS[g]
+        def quantise(a, b):
             nc.vector.quantize_mx(out=codes(a, b), scales=scales[:, a:b], in_=group_view(a, b))
 
         for t in range(4):
@@ -112,8 +111,8 @@ def tile_picked_gmem_tanh_e_kernel(tc, xT, mem, w1_words, w1_scales, w2_words, w
                     gather_vector(t, a, b)
                 for a, b in GROUPS[2:]:
                     gather_scalar(t, a, b)
-        for g in range(4):
-            quantise(g)
+        for a, b in STEPS:
+            quantise(a, b)
 
         cand = sb.tile([P, S], F32, name="cand")
         keep = sb.tile([P, S], F32, name="keep")

@@ -17,13 +17,12 @@ ACT = mybir.ActivationFunctionType
 ALU = mybir.AluOpType
 
 P = 128
-GROUPS = ((0, 256), (256, 512), (512, 768), (768, 1024))
-STEPS = ((0, 128), (128, 256)) + GROUPS[1:]
 PLANES = (0, 2, 1, 3)
-SPLITS = (352, 352, 288, 512)
+SPLITS = (352, 352, 288)
 PIECES = ((0, 1280, 2048), (0, 1280, 2048), (0, 1280, 2048), (0, 1152, 1792, 2048))
-POOL = 512
 FIRST = 256
+FETCH = 640
+FILL = 448
 
 
 def tile_picked_gmem_tanh_e_kernel(tc, xT, mem, w1_words, w1_scales, w2_words, w2_scales, offs, slot, out):
@@ -55,13 +54,14 @@ def tile_picked_gmem_tanh_e_kernel(tc, xT, mem, w1_words, w1_scales, w2_words, w
         for t in range(4):
             for a, b in zip(PIECES[t], PIECES[t][1:]):
                 nc.sync.dma_start(out=raw[t][:, a:b], in_=x_rows[:, PLANES[t], a:b])
+                if t == 2 and a == 0:
+                    load_scales(1, w2_scales, nc.sync)
             if t == 0:
                 nc.sync.dma_start(offs_sb[:], offs)
         load_words(0, w1_words)
+        load_words(1, w2_words)
         nc.sync.dma_start(out=memory[:], in_=mem)
         nc.sync.dma_start(slot_sb[:], slot)
-        load_words(1, w2_words)
-        load_scales(1, w2_scales, nc.sync)
 
         warm = sb.tile([P, 2], F32, name="warm")
         nc.vector.memset(warm[:, 0:1], 0.0)
@@ -107,17 +107,16 @@ def tile_picked_gmem_tanh_e_kernel(tc, xT, mem, w1_words, w1_scales, w2_words, w
                 gather_vector(t, 0, SPLITS[t])
                 gather_scalar(t, SPLITS[t], S)
             else:
-                for a, b in GROUPS[:2]:
-                    gather_vector(t, a, b)
-                for a, b in GROUPS[2:]:
-                    gather_scalar(t, a, b)
-        for a, b in STEPS:
-            quantise(a, b)
+                for a in (0, 256):
+                    gather_vector(t, a, a + 256)
+                    gather_scalar(t, a + 512, a + 768)
 
         cand = sb.tile([P, S], F32, name="cand")
         keep = sb.tile([P, S], F32, name="keep")
         diff = sb.tile([P, S], F32, name="diff")
         step = sb.tile([P, S], F32, name="step")
+        old = sb.tile([P, S], F32, name="old")
+        fresh = sb.tile([P, FIRST], F32, name="fresh")
 
         def multiply(acc, i, a, b):
             nc.tensor.matmul_mx(
@@ -136,35 +135,41 @@ def tile_picked_gmem_tanh_e_kernel(tc, xT, mem, w1_words, w1_scales, w2_words, w
         def gate(acc, a, b):
             nc.scalar.activation(out=keep[:, a:b], in_=acc, func=ACT.Sigmoid, scale=-1.0)
 
-        for a, b in STEPS[:4]:
-            acc = ps.tile([P, b - a], F32, name="acc0_%d" % a)
-            multiply(acc[:], 0, a, b)
-            candidate(acc[:], a, b)
-        shared = ps.tile([P, 512], F32, name="shared")
-        multiply(shared[:, 256:512], 0, 768, S)
-        multiply(shared[:, 0:256], 1, 0, 256)
-        second = ps.tile([P, 256], F32, name="second")
-        multiply(second[:], 1, 256, 512)
-        third = ps.tile([P, 512], F32, name="third")
-        multiply(third[:], 1, 512, S)
-        gate(shared[:, 0:256], 0, 256)
-        candidate(shared[:, 256:512], 768, S)
-        gate(second[:], 256, 512)
-        gate(third[:], 512, S)
+        def product(i, a, b):
+            acc = ps.tile([P, b - a], F32, name="acc%d_%d" % (i, a))
+            multiply(acc[:], i, a, b)
+            (candidate, gate)[i](acc[:], a, b)
 
-        fresh = sb.tile([P, FIRST], F32, name="fresh")
+        def fetch_vector(a, b):
+            nc.vector.tensor_copy(out=old[:, a:b], in_=memory[:].indirect(entries(slot_sb, a, b)))
 
         def subtract(a, b):
             nc.vector.tensor_tensor(diff[:, a:b], memory[:].indirect(entries(slot_sb, a, b)), cand[:, a:b], ALU.subtract)
 
-        for a, b in STEPS[:4]:
-            subtract(a, b)
-        early = step[:, POOL : POOL + FIRST]
-        nc.vector.tensor_tensor(early, diff[:, 0:FIRST], keep[:, 0:FIRST], ALU.mult)
-        subtract(768, S)
-        nc.vector.tensor_tensor(fresh[:], early, cand[:, 0:FIRST], ALU.add)
-        nc.vector.tensor_tensor(step[:, FIRST:POOL], diff[:, FIRST:POOL], keep[:, FIRST:POOL], ALU.mult)
-        nc.vector.tensor_copy(out=memory[:].indirect(entries(slot_sb, 0, FIRST)), in_=fresh[:])
-        nc.gpsimd.tensor_tensor(step[:, POOL:S], diff[:, POOL:S], keep[:, POOL:S], ALU.mult)
+        def scale_down(a, b):
+            nc.vector.tensor_tensor(step[:, a:b], diff[:, a:b], keep[:, a:b], ALU.mult)
+
+        for a, b in ((0, 128), (128, 256), (256, 512), (512, 768), (768, 1024)):
+            quantise(a, b)
+        for i, a, b in ((0, 0, 128), (0, 128, 256), (1, 0, 256), (0, 256, 512), (1, 256, 512), (0, 512, 768)):
+            product(i, a, b)
+        shared = ps.tile([P, 512], F32, name="shared")
+        multiply(shared[:, 0:256], 1, 512, 768)
+        multiply(shared[:, 256:512], 0, 768, S)
+        gate(shared[:, 0:256], 512, 768)
+        candidate(shared[:, 256:512], 768, S)
+        product(1, 768, S)
+        nc.scalar.activation(out=old[:, FETCH:S], in_=memory[:].indirect(entries(slot_sb, FETCH, S)), func=ACT.Copy)
+
+        subtract(0, FIRST)
+        fetch_vector(FIRST, FILL)
+        scale_down(0, FIRST)
+        fetch_vector(FILL, FETCH)
+        nc.vector.tensor_tensor(fresh[:], step[:, 0:FIRST], cand[:, 0:FIRST], ALU.add)
+        nc.scalar.activation(out=memory[:].indirect(entries(slot_sb, 0, FIRST)), in_=fresh[:], func=ACT.Copy)
+        for a, b in ((FIRST, 640), (640, S)):
+            nc.vector.tensor_tensor(diff[:, a:b], old[:, a:b], cand[:, a:b], ALU.subtract)
+        for a, b in ((FIRST, 640), (640, S)):
+            scale_down(a, b)
         nc.vector.tensor_tensor(memory[:].indirect(entries(slot_sb, FIRST, S)), step[:, FIRST:S], cand[:, FIRST:S], ALU.add)
         nc.sync.dma_start(out=out, in_=memory[:])

@@ -17,12 +17,11 @@ ACT = mybir.ActivationFunctionType
 ALU = mybir.AluOpType
 
 P = 128
-PLANES = (0, 2, 1, 3)
-SPLITS = (352, 352, 288)
-PIECES = ((0, 1280, 2048), (0, 1280, 2048), (0, 1280, 2048), (0, 1152, 1792, 2048))
+OWN = 256
+PIECES = ((256, 512), (512, 768), (768, 1024))
 FIRST = 256
-FETCH = 640
-FILL = 448
+FETCH = 512
+FILL = 384
 
 
 def tile_picked_gmem_tanh_e_kernel(tc, xT, mem, w1_words, w1_scales, w2_words, w2_scales, offs, slot, out):
@@ -52,16 +51,14 @@ def tile_picked_gmem_tanh_e_kernel(tc, xT, mem, w1_words, w1_scales, w2_words, w
         load_scales(0, w1_scales, nc.scalar)
         raw = [sb.tile([P, T], F32, name="raw%d" % t) for t in range(4)]
         for t in range(4):
-            for a, b in zip(PIECES[t], PIECES[t][1:]):
-                nc.sync.dma_start(out=raw[t][:, a:b], in_=x_rows[:, PLANES[t], a:b])
-                if t == 2 and a == 0:
-                    load_scales(1, w2_scales, nc.sync)
+            nc.sync.dma_start(out=raw[t][:], in_=x_rows[:, t, :])
             if t == 0:
                 nc.sync.dma_start(offs_sb[:], offs)
         load_words(0, w1_words)
-        load_words(1, w2_words)
         nc.sync.dma_start(out=memory[:], in_=mem)
         nc.sync.dma_start(slot_sb[:], slot)
+        load_words(1, w2_words)
+        load_scales(1, w2_scales, nc.sync)
 
         warm = sb.tile([P, 2], F32, name="warm")
         nc.vector.memset(warm[:, 0:1], 0.0)
@@ -70,26 +67,24 @@ def tile_picked_gmem_tanh_e_kernel(tc, xT, mem, w1_words, w1_scales, w2_words, w
         def entries(lst, a, b):
             return lst[:, a // 16 : b // 16]
 
-        rounded = [sb.tile([P, T], BF16, name="rounded%d" % t) for t in range(2)] * 2
         grouped = sb.tile([P, 4 * S], BF16, name="grouped", align_bytes=64)
 
         def group_view(a, b):
             return grouped[:, 4 * a : 4 * b]
 
-        def cast(t):
-            for a, b in zip(PIECES[t], PIECES[t][1:]):
-                if t == 0 and b == T:
-                    nc.scalar.activation(out=rounded[t][:, b - 256 : b], in_=raw[t][:, b - 256 : b], func=ACT.Copy)
-                    b = b - 256
-                nc.vector.tensor_copy(out=rounded[t][:, a:b], in_=raw[t][:, a:b])
-
         def gather_vector(t, a, b):
-            dst = group_view(a, b).rearrange("p (n t) -> p n t", t=4)[:, :, PLANES[t]]
+            dst = group_view(a, b).rearrange("p (n t) -> p n t", t=4)[:, :, t]
             nc.vector.tensor_copy(out=dst, in_=raw[t][:].indirect(entries(offs_sb, a, b)))
 
+        stretches = (((OWN, S),), PIECES)
+        pairs = {(h, a): sb.tile([P, 2, b - a], BF16, name="pair%d_%d" % (h, a)) for h in range(2) for a, b in stretches[h]}
+
         def gather_scalar(t, a, b):
-            dst = group_view(a, b).rearrange("p (n t) -> p n t", t=4)[:, :, PLANES[t]]
-            nc.scalar.activation(out=dst, in_=rounded[t][:].indirect(entries(offs_sb, a, b)), func=ACT.Copy)
+            nc.scalar.activation(out=pairs[t // 2, a][:, t % 2, :], in_=raw[t][:].indirect(entries(offs_sb, a, b)), func=ACT.Copy)
+
+        def weave(h, a, b):
+            dst = group_view(a, b).rearrange("p (n t) -> p n t", t=4)[:, :, 2 * h : 2 * h + 2]
+            nc.vector.tensor_copy(out=dst, in_=pairs[h, a][:].rearrange("p j n -> p n j"))
 
         codes_sb = sb.tile([P, S], U32, name="codes_sb", align_bytes=64)
 
@@ -102,14 +97,11 @@ def tile_picked_gmem_tanh_e_kernel(tc, xT, mem, w1_words, w1_scales, w2_words, w
             nc.vector.quantize_mx(out=codes(a, b), scales=scales[:, a:b], in_=group_view(a, b))
 
         for t in range(4):
-            cast(t)
-            if t < 3:
-                gather_vector(t, 0, SPLITS[t])
-                gather_scalar(t, SPLITS[t], S)
-            else:
-                for a in (0, 256):
-                    gather_vector(t, a, a + 256)
-                    gather_scalar(t, a + 512, a + 768)
+            gather_vector(t, 0, OWN)
+            for a, b in stretches[t // 2]:
+                gather_scalar(t, a, b)
+            if t == 1:
+                weave(0, OWN, S)
 
         cand = sb.tile([P, S], F32, name="cand")
         keep = sb.tile([P, S], F32, name="keep")
@@ -149,17 +141,24 @@ def tile_picked_gmem_tanh_e_kernel(tc, xT, mem, w1_words, w1_scales, w2_words, w
         def scale_down(a, b):
             nc.vector.tensor_tensor(step[:, a:b], diff[:, a:b], keep[:, a:b], ALU.mult)
 
-        for a, b in ((0, 128), (128, 256), (256, 512), (512, 768), (768, 1024)):
-            quantise(a, b)
-        for i, a, b in ((0, 0, 128), (0, 128, 256), (1, 0, 256), (0, 256, 512), (1, 256, 512), (0, 512, 768)):
-            product(i, a, b)
-        shared = ps.tile([P, 512], F32, name="shared")
-        multiply(shared[:, 0:256], 1, 512, 768)
-        multiply(shared[:, 256:512], 0, 768, S)
-        gate(shared[:, 0:256], 512, 768)
-        candidate(shared[:, 256:512], 768, S)
-        product(1, 768, S)
+        weave(1, 256, 512)
+        quantise(0, 128)
+        quantise(128, 256)
+        weave(1, 512, 768)
+        quantise(256, 512)
+        weave(1, 768, 1024)
+        quantise(512, 768)
+        quantise(768, 1024)
+        product(0, 0, 128)
+        product(0, 128, 256)
         nc.scalar.activation(out=old[:, FETCH:S], in_=memory[:].indirect(entries(slot_sb, FETCH, S)), func=ACT.Copy)
+        for a in (0, 256, 512):
+            shared = ps.tile([P, 512], F32, name="shared%d" % a)
+            multiply(shared[:, 0:256], 1, a, a + 256)
+            multiply(shared[:, 256:512], 0, a + 256, a + 512)
+            gate(shared[:, 0:256], a, a + 256)
+            candidate(shared[:, 256:512], a + 256, a + 512)
+        product(1, 768, S)
 
         subtract(0, FIRST)
         fetch_vector(FIRST, FILL)

@@ -20,7 +20,7 @@ P = 128
 OWN = 256
 PIECES = ((256, 512), (512, 768), (768, 1024))
 FIRST = 256
-FETCH = 512
+FETCH = 448
 FILL = 384
 
 
@@ -76,7 +76,7 @@ def tile_picked_gmem_tanh_e_kernel(tc, xT, mem, w1_words, w1_scales, w2_words, w
             dst = group_view(a, b).rearrange("p (n t) -> p n t", t=4)[:, :, t]
             nc.vector.tensor_copy(out=dst, in_=raw[t][:].indirect(entries(offs_sb, a, b)))
 
-        stretches = (((OWN, S),), PIECES)
+        stretches = (PIECES, PIECES)
         pairs = {(h, a): sb.tile([P, 2, b - a], BF16, name="pair%d_%d" % (h, a)) for h in range(2) for a, b in stretches[h]}
 
         def gather_scalar(t, a, b):
@@ -100,8 +100,8 @@ def tile_picked_gmem_tanh_e_kernel(tc, xT, mem, w1_words, w1_scales, w2_words, w
             gather_vector(t, 0, OWN)
             for a, b in stretches[t // 2]:
                 gather_scalar(t, a, b)
-            if t == 1:
-                weave(0, OWN, S)
+                if t == 1:
+                    weave(0, a, b)
 
         cand = sb.tile([P, S], F32, name="cand")
         keep = sb.tile([P, S], F32, name="keep")
@@ -142,33 +142,31 @@ def tile_picked_gmem_tanh_e_kernel(tc, xT, mem, w1_words, w1_scales, w2_words, w
             nc.vector.tensor_tensor(step[:, a:b], diff[:, a:b], keep[:, a:b], ALU.mult)
 
         weave(1, 256, 512)
-        quantise(0, 128)
-        quantise(128, 256)
+        quantise(0, 256)
         weave(1, 512, 768)
         quantise(256, 512)
         weave(1, 768, 1024)
         quantise(512, 768)
         quantise(768, 1024)
-        product(0, 0, 128)
-        product(0, 128, 256)
+        product(0, 0, 256)
         nc.scalar.activation(out=old[:, FETCH:S], in_=memory[:].indirect(entries(slot_sb, FETCH, S)), func=ACT.Copy)
-        for a in (0, 256, 512):
+        product(1, 0, 256)
+        for a, b in PIECES:
             shared = ps.tile([P, 512], F32, name="shared%d" % a)
-            multiply(shared[:, 0:256], 1, a, a + 256)
-            multiply(shared[:, 256:512], 0, a + 256, a + 512)
-            gate(shared[:, 0:256], a, a + 256)
-            candidate(shared[:, 256:512], a + 256, a + 512)
-        product(1, 768, S)
+            multiply(shared[:, 256:512], 1, a, b)
+            multiply(shared[:, 0:256], 0, a, b)
+            candidate(shared[:, 0:256], a, b)
+            gate(shared[:, 256:512], a, b)
 
         subtract(0, FIRST)
         fetch_vector(FIRST, FILL)
         scale_down(0, FIRST)
-        fetch_vector(FILL, FETCH)
+        subtract(FILL, FETCH)
         nc.vector.tensor_tensor(fresh[:], step[:, 0:FIRST], cand[:, 0:FIRST], ALU.add)
         nc.scalar.activation(out=memory[:].indirect(entries(slot_sb, 0, FIRST)), in_=fresh[:], func=ACT.Copy)
-        for a, b in ((FIRST, 640), (640, S)):
+        for a, b in ((FIRST, FILL), (FETCH, S)):
             nc.vector.tensor_tensor(diff[:, a:b], old[:, a:b], cand[:, a:b], ALU.subtract)
-        for a, b in ((FIRST, 640), (640, S)):
+        for a, b in ((FIRST, FETCH), (FETCH, S)):
             scale_down(a, b)
         nc.vector.tensor_tensor(memory[:].indirect(entries(slot_sb, FIRST, S)), step[:, FIRST:S], cand[:, FIRST:S], ALU.add)
         nc.sync.dma_start(out=out, in_=memory[:])

@@ -20,8 +20,8 @@ P = 128
 OWN = 256
 PIECES = ((256, 512), (512, 768), (768, 1024))
 FIRST = 256
-FETCH = 448
-FILL = 384
+CUT = 704
+LATE = 768
 
 
 def tile_picked_gmem_tanh_e_kernel(tc, xT, mem, w1_words, w1_scales, w2_words, w2_scales, offs, slot, out):
@@ -33,6 +33,7 @@ def tile_picked_gmem_tanh_e_kernel(tc, xT, mem, w1_words, w1_scales, w2_words, w
         offs_sb = sb.tile([P, S // 16], U16, name="offs_sb")
         slot_sb = sb.tile([P, S // 16], U16, name="slot_sb")
         memory = sb.tile([P, U], F32, name="memory")
+        lookup = sb.tile([P, U], F32, name="lookup")
         x_rows = xT.rearrange("(p j) t -> p j t", j=4)
         w_words = [sb.tile([P, 2 * N], U8, name="w_words%d" % i, align_bytes=64) for i in range(2)]
         w_scales = sb.tile([P, 2 * N], U8, name="w_scales", align_bytes=64)
@@ -59,6 +60,7 @@ def tile_picked_gmem_tanh_e_kernel(tc, xT, mem, w1_words, w1_scales, w2_words, w
         nc.sync.dma_start(slot_sb[:], slot)
         load_words(1, w2_words)
         load_scales(1, w2_scales, nc.sync)
+        nc.sync.dma_start(out=lookup[:], in_=mem)
 
         warm = sb.tile([P, 2], F32, name="warm")
         nc.vector.memset(warm[:, 0:1], 0.0)
@@ -86,10 +88,11 @@ def tile_picked_gmem_tanh_e_kernel(tc, xT, mem, w1_words, w1_scales, w2_words, w
             dst = group_view(a, b).rearrange("p (n t) -> p n t", t=4)[:, :, 2 * h : 2 * h + 2]
             nc.vector.tensor_copy(out=dst, in_=pairs[h, a][:].rearrange("p j n -> p n j"))
 
-        codes_sb = sb.tile([P, S], U32, name="codes_sb", align_bytes=64)
+        codes_sb = {0: sb.tile([P, LATE], U32, name="codes_sb", align_bytes=64)}
 
         def codes(a, b):
-            return codes_sb[:, a:b].bitcast(FP8X4)
+            home = LATE if a >= LATE else 0
+            return codes_sb[home][:, a - home : b - home].bitcast(FP8X4)
 
         scales = sb.tile([P, S], U8, name="scales", align_bytes=64)
 
@@ -105,10 +108,10 @@ def tile_picked_gmem_tanh_e_kernel(tc, xT, mem, w1_words, w1_scales, w2_words, w
 
         cand = sb.tile([P, S], F32, name="cand")
         keep = sb.tile([P, S], F32, name="keep")
-        diff = sb.tile([P, S], F32, name="diff")
         step = sb.tile([P, S], F32, name="step")
-        old = sb.tile([P, S], F32, name="old")
-        fresh = sb.tile([P, FIRST], F32, name="fresh")
+        old = sb.tile([P, LATE - FIRST], F32, name="old")
+        fresh = sb.tile([P, CUT - FIRST], F32, name="fresh")
+        opening = sb.tile([P, FIRST], F32, name="opening")
 
         def multiply(acc, i, a, b):
             nc.tensor.matmul_mx(
@@ -132,41 +135,53 @@ def tile_picked_gmem_tanh_e_kernel(tc, xT, mem, w1_words, w1_scales, w2_words, w
             multiply(acc[:], i, a, b)
             (candidate, gate)[i](acc[:], a, b)
 
-        def fetch_vector(a, b):
-            nc.vector.tensor_copy(out=old[:, a:b], in_=memory[:].indirect(entries(slot_sb, a, b)))
-
-        def subtract(a, b):
-            nc.vector.tensor_tensor(diff[:, a:b], memory[:].indirect(entries(slot_sb, a, b)), cand[:, a:b], ALU.subtract)
-
-        def scale_down(a, b):
-            nc.vector.tensor_tensor(step[:, a:b], diff[:, a:b], keep[:, a:b], ALU.mult)
-
         weave(1, 256, 512)
         quantise(0, 256)
         weave(1, 512, 768)
         quantise(256, 512)
         weave(1, 768, 1024)
         quantise(512, 768)
-        quantise(768, 1024)
-        product(0, 0, 256)
-        nc.scalar.activation(out=old[:, FETCH:S], in_=memory[:].indirect(entries(slot_sb, FETCH, S)), func=ACT.Copy)
-        product(1, 0, 256)
-        for a, b in PIECES:
+        product(0, 0, FIRST)
+        nc.scalar.activation(out=old[:], in_=memory[:].indirect(entries(slot_sb, FIRST, LATE)), func=ACT.Copy)
+        product(1, 0, FIRST)
+        for a, b in PIECES[:2]:
             shared = ps.tile([P, 512], F32, name="shared%d" % a)
             multiply(shared[:, 256:512], 1, a, b)
             multiply(shared[:, 0:256], 0, a, b)
             candidate(shared[:, 0:256], a, b)
             gate(shared[:, 256:512], a, b)
 
-        subtract(0, FIRST)
-        fetch_vector(FIRST, FILL)
-        scale_down(0, FIRST)
-        subtract(FILL, FETCH)
-        nc.vector.tensor_tensor(fresh[:], step[:, 0:FIRST], cand[:, 0:FIRST], ALU.add)
-        nc.scalar.activation(out=memory[:].indirect(entries(slot_sb, 0, FIRST)), in_=fresh[:], func=ACT.Copy)
-        for a, b in ((FIRST, FILL), (FETCH, S)):
-            nc.vector.tensor_tensor(diff[:, a:b], old[:, a:b], cand[:, a:b], ALU.subtract)
-        for a, b in ((FIRST, FETCH), (FETCH, S)):
-            scale_down(a, b)
-        nc.vector.tensor_tensor(memory[:].indirect(entries(slot_sb, FIRST, S)), step[:, FIRST:S], cand[:, FIRST:S], ALU.add)
+        half = FIRST // 2
+        halves = (slice(0, half), slice(half, FIRST))
+        diffs = [sb.tile([P, half], F32, name="diff%d" % h.start, align_bytes=64) for h in halves]
+        for diff, h in zip(diffs, halves):
+            nc.vector.tensor_tensor(diff[:], memory[:].indirect(entries(slot_sb, h.start, h.stop)), cand[:, h], ALU.subtract)
+        for diff, h in zip(diffs, halves):
+            nc.vector.tensor_tensor(step[:, h], diff[:], keep[:, h], ALU.mult)
+        for h in halves:
+            nc.vector.tensor_tensor(opening[:, h], step[:, h], cand[:, h], ALU.add)
+        nc.scalar.activation(out=memory[:].indirect(entries(slot_sb, 0, FIRST)), in_=opening[:], func=ACT.Copy)
+
+        codes_sb[LATE] = sb.tile([P, S - LATE], U32, name="diff%d" % half, align_bytes=64)
+        quantise(LATE, S)
+        product(0, LATE, S)
+        old_late = sb.tile([P, S - LATE], F32, name="opening")
+        nc.scalar.activation(out=old_late[:], in_=lookup[:].indirect(entries(slot_sb, LATE, S)), func=ACT.Copy)
+        product(1, LATE, S)
+
+        middle = sb.tile([P, CUT - FIRST], F32, name="middle")
+        diff = sb.tile([P, S - CUT], F32, name="diff_late")
+        steps = ((FIRST, 512), (512, CUT))
+        for a, b in steps:
+            nc.vector.tensor_tensor(middle[:, a - FIRST : b - FIRST], old[:, a - FIRST : b - FIRST], cand[:, a:b], ALU.subtract)
+        nc.vector.tensor_tensor(diff[:, 0 : LATE - CUT], old[:, CUT - FIRST :], cand[:, CUT:LATE], ALU.subtract)
+        for a, b in steps:
+            nc.vector.tensor_tensor(step[:, a:b], middle[:, a - FIRST : b - FIRST], keep[:, a:b], ALU.mult)
+        for a, b in steps:
+            nc.vector.tensor_tensor(fresh[:, a - FIRST : b - FIRST], step[:, a:b], cand[:, a:b], ALU.add)
+        nc.vector.tensor_copy(out=memory[:].indirect(entries(slot_sb, FIRST, CUT)), in_=fresh[:])
+
+        nc.gpsimd.tensor_tensor(diff[:, LATE - CUT :], old_late[:], cand[:, LATE:S], ALU.subtract)
+        nc.gpsimd.tensor_tensor(step[:, CUT:S], diff[:], keep[:, CUT:S], ALU.mult)
+        nc.vector.tensor_tensor(memory[:].indirect(entries(slot_sb, CUT, S)), step[:, CUT:S], cand[:, CUT:S], ALU.add)
         nc.sync.dma_start(out=out, in_=memory[:])

@@ -56,10 +56,10 @@ def tile_picked_gmem_tanh_e_kernel(tc, xT, mem, w1_words, w1_scales, w2_words, w
             if t == 0:
                 nc.sync.dma_start(offs_sb[:], offs)
         load_words(0, w1_words)
+        load_scales(1, w2_scales, nc.sync)
         nc.sync.dma_start(out=memory[:], in_=mem)
         nc.sync.dma_start(slot_sb[:], slot)
         load_words(1, w2_words)
-        load_scales(1, w2_scales, nc.sync)
         nc.sync.dma_start(out=lookup[:], in_=mem)
 
         warm = sb.tile([P, 2], F32, name="warm")
@@ -109,7 +109,7 @@ def tile_picked_gmem_tanh_e_kernel(tc, xT, mem, w1_words, w1_scales, w2_words, w
         cand = sb.tile([P, S], F32, name="cand")
         keep = sb.tile([P, S], F32, name="keep")
         step = sb.tile([P, S], F32, name="step")
-        old = sb.tile([P, LATE - FIRST], F32, name="old")
+        old = sb.tile([P, CUT - FIRST], F32, name="old")
         fresh = sb.tile([P, CUT - FIRST], F32, name="fresh")
         opening = sb.tile([P, FIRST], F32, name="opening")
 
@@ -142,7 +142,7 @@ def tile_picked_gmem_tanh_e_kernel(tc, xT, mem, w1_words, w1_scales, w2_words, w
         weave(1, 768, 1024)
         quantise(512, 768)
         product(0, 0, FIRST)
-        nc.scalar.activation(out=old[:], in_=memory[:].indirect(entries(slot_sb, FIRST, LATE)), func=ACT.Copy)
+        nc.scalar.activation(out=old[:], in_=memory[:].indirect(entries(slot_sb, FIRST, CUT)), func=ACT.Copy)
         product(1, 0, FIRST)
         for a, b in PIECES[:2]:
             shared = ps.tile([P, 512], F32, name="shared%d" % a)
@@ -165,8 +165,8 @@ def tile_picked_gmem_tanh_e_kernel(tc, xT, mem, w1_words, w1_scales, w2_words, w
         codes_sb[LATE] = sb.tile([P, S - LATE], U32, name="diff%d" % half, align_bytes=64)
         quantise(LATE, S)
         product(0, LATE, S)
-        old_late = sb.tile([P, S - LATE], F32, name="opening")
-        nc.scalar.activation(out=old_late[:], in_=lookup[:].indirect(entries(slot_sb, LATE, S)), func=ACT.Copy)
+        old_late = sb.tile([P, S - CUT], F32, name="opening")
+        nc.scalar.activation(out=old_late[:], in_=lookup[:].indirect(entries(slot_sb, CUT, S)), func=ACT.Copy)
         product(1, LATE, S)
 
         middle = sb.tile([P, CUT - FIRST], F32, name="middle")
@@ -174,14 +174,13 @@ def tile_picked_gmem_tanh_e_kernel(tc, xT, mem, w1_words, w1_scales, w2_words, w
         steps = ((FIRST, 512), (512, CUT))
         for a, b in steps:
             nc.vector.tensor_tensor(middle[:, a - FIRST : b - FIRST], old[:, a - FIRST : b - FIRST], cand[:, a:b], ALU.subtract)
-        nc.vector.tensor_tensor(diff[:, 0 : LATE - CUT], old[:, CUT - FIRST :], cand[:, CUT:LATE], ALU.subtract)
         for a, b in steps:
             nc.vector.tensor_tensor(step[:, a:b], middle[:, a - FIRST : b - FIRST], keep[:, a:b], ALU.mult)
         for a, b in steps:
             nc.vector.tensor_tensor(fresh[:, a - FIRST : b - FIRST], step[:, a:b], cand[:, a:b], ALU.add)
         nc.vector.tensor_copy(out=memory[:].indirect(entries(slot_sb, FIRST, CUT)), in_=fresh[:])
 
-        nc.gpsimd.tensor_tensor(diff[:, LATE - CUT :], old_late[:], cand[:, LATE:S], ALU.subtract)
+        nc.gpsimd.tensor_tensor(diff[:], old_late[:], cand[:, CUT:S], ALU.subtract)
         nc.gpsimd.tensor_tensor(step[:, CUT:S], diff[:], keep[:, CUT:S], ALU.mult)
         nc.vector.tensor_tensor(memory[:].indirect(entries(slot_sb, CUT, S)), step[:, CUT:S], cand[:, CUT:S], ALU.add)
         nc.sync.dma_start(out=out, in_=memory[:])

@@ -37,26 +37,31 @@ def tile_picked_gmem_tanh_e_kernel(tc, xT, mem, w1_words, w1_scales, w2_words, w
         x_rows = xT.rearrange("(p j) t -> p j t", j=4)
         w_words = [sb.tile([P, 2 * N], U8, name="w_words%d" % i, align_bytes=64) for i in range(2)]
         w_scales = sb.tile([P, 2 * N], U8, name="w_scales", align_bytes=64)
-        nc.gpsimd.memset(w_scales[:].bitcast(I32), 0)
+        nc.vector.memset(w_scales[:].bitcast(I32), 0)
 
         def load_words(i, words):
             nc.sync.dma_start(out=w_words[i][:].bitcast(I32), in_=words[0].bitcast(I32))
 
-        def load_scales(i, scales, queue):
+        def load_scales(i, scales):
+            staged = sb.tile([4, 4 * N], U8, name="staged%d" % i)
+            nc.scalar.dma_start(
+                out=staged[:].bitcast(I32).rearrange("r (q n) -> r q n", q=4),
+                in_=scales[0].bitcast(I32).rearrange("(q r) n -> r q n", r=4),
+            )
             for q in range(4):
-                queue.dma_start(
+                nc.vector.tensor_copy(
                     out=w_scales[32 * q : 32 * q + 4, i * N : (i + 1) * N].bitcast(I32),
-                    in_=scales[0, 4 * q : 4 * q + 4, :].bitcast(I32),
+                    in_=staged[:, q * N : (q + 1) * N].bitcast(I32),
                 )
 
-        load_scales(0, w1_scales, nc.scalar)
+        load_scales(0, w1_scales)
+        load_scales(1, w2_scales)
         raw = [sb.tile([P, T], F32, name="raw%d" % t) for t in range(4)]
         for t in range(4):
             nc.sync.dma_start(out=raw[t][:], in_=x_rows[:, t, :])
             if t == 0:
                 nc.sync.dma_start(offs_sb[:], offs)
         load_words(0, w1_words)
-        load_scales(1, w2_scales, nc.sync)
         nc.sync.dma_start(out=memory[:], in_=mem)
         nc.sync.dma_start(slot_sb[:], slot)
         load_words(1, w2_words)

from contextlib import ExitStack

import concourse.mybir as mybir

K, T, S, N, U = 512, 2048, 1024, 128, 2048
FLOPS = 2 * 2 * K * N * S

F32 = mybir.dt.float32
BF16 = mybir.dt.bfloat16
I32 = mybir.dt.int32
U32 = mybir.dt.uint32
U16 = mybir.dt.uint16
U8 = mybir.dt.uint8
FP8X4 = mybir.dt.float8_e4m3fn_x4
FP4X4 = mybir.dt.float4_e2m1fn_x4
ACT = mybir.ActivationFunctionType
ALU = mybir.AluOpType

P = 128
OWN = 256
PIECES = ((256, 512), (512, 768), (768, 1024))
FIRST = 256
CUT = 704
LATE = 768


def tile_picked_gmem_tanh_e_kernel(tc, xT, mem, w1_words, w1_scales, w2_words, w2_scales, offs, slot, out):
    nc = tc.nc
    with ExitStack() as ctx:
        sb = ctx.enter_context(tc.tile_pool(name="sb", bufs=1))
        ps = ctx.enter_context(tc.psum_pool(name="ps", bufs=1))

        offs_sb = sb.tile([P, S // 16], U16, name="offs_sb")
        slot_sb = sb.tile([P, S // 16], U16, name="slot_sb")
        memory = sb.tile([P, U], F32, name="memory")
        lookup = sb.tile([P, U], F32, name="lookup")
        x_rows = xT.rearrange("(p j) t -> p j t", j=4)
        w_words = [sb.tile([P, 2 * N], U8, name="w_words%d" % i, align_bytes=64) for i in range(2)]
        w_scales = sb.tile([P, 2 * N], U8, name="w_scales", align_bytes=64)
        nc.vector.memset(w_scales[:].bitcast(I32), 0)

        def load_words(i, words):
            nc.sync.dma_start(out=w_words[i][:].bitcast(I32), in_=words[0].bitcast(I32))

        def load_scales(i, scales):
            staged = sb.tile([4, 4 * N], U8, name="staged%d" % i)
            nc.scalar.dma_start(
                out=staged[:].bitcast(I32).rearrange("r (q n) -> r q n", q=4),
                in_=scales[0].bitcast(I32).rearrange("(q r) n -> r q n", r=4),
            )
            for q in range(4):
                nc.vector.tensor_copy(
                    out=w_scales[32 * q : 32 * q + 4, i * N : (i + 1) * N].bitcast(I32),
                    in_=staged[:, q * N : (q + 1) * N].bitcast(I32),
                )

        load_scales(0, w1_scales)
        load_scales(1, w2_scales)
        raw = [sb.tile([P, T], F32, name="raw%d" % t) for t in range(4)]
        for t in range(4):
            nc.sync.dma_start(out=raw[t][:], in_=x_rows[:, t, :])
            if t == 0:
                nc.sync.dma_start(offs_sb[:], offs)
        load_words(0, w1_words)
        nc.sync.dma_start(out=memory[:], in_=mem)
        nc.sync.dma_start(slot_sb[:], slot)
        load_words(1, w2_words)
        nc.sync.dma_start(out=lookup[:], in_=mem)

        warm = sb.tile([P, 2], F32, name="warm")
        nc.vector.memset(warm[:, 0:1], 0.0)
        nc.scalar.activation(out=warm[:, 1:2], in_=warm[:, 0:1], func=ACT.Sigmoid)

        def entries(lst, a, b):
            return lst[:, a // 16 : b // 16]

        grouped = sb.tile([P, 4 * S], BF16, name="grouped", align_bytes=64)

        def group_view(a, b):
            return grouped[:, 4 * a : 4 * b]

        def gather_vector(t, a, b):
            dst = group_view(a, b).rearrange("p (n t) -> p n t", t=4)[:, :, t]
            nc.vector.tensor_copy(out=dst, in_=raw[t][:].indirect(entries(offs_sb, a, b)))

        stretches = (PIECES, PIECES)
        pairs = {(h, a): sb.tile([P, 2, b - a], BF16, name="pair%d_%d" % (h, a)) for h in range(2) for a, b in stretches[h]}

        def gather_scalar(t, a, b):
            nc.scalar.activation(out=pairs[t // 2, a][:, t % 2, :], in_=raw[t][:].indirect(entries(offs_sb, a, b)), func=ACT.Copy)

        def weave(h, a, b):
            dst = group_view(a, b).rearrange("p (n t) -> p n t", t=4)[:, :, 2 * h : 2 * h + 2]
            nc.vector.tensor_copy(out=dst, in_=pairs[h, a][:].rearrange("p j n -> p n j"))

        codes_sb = {0: sb.tile([P, LATE], U32, name="codes_sb", align_bytes=64)}

        def codes(a, b):
            home = LATE if a >= LATE else 0
            return codes_sb[home][:, a - home : b - home].bitcast(FP8X4)

        scales = sb.tile([P, S], U8, name="scales", align_bytes=64)

        def quantise(a, b):
            nc.vector.quantize_mx(out=codes(a, b), scales=scales[:, a:b], in_=group_view(a, b))

        for t in range(4):
            gather_vector(t, 0, OWN)
            for a, b in stretches[t // 2]:
                gather_scalar(t, a, b)
                if t == 1:
                    weave(0, a, b)

        cand = sb.tile([P, S], F32, name="cand")
        keep = sb.tile([P, S], F32, name="keep")
        step = sb.tile([P, S], F32, name="step")
        old = sb.tile([P, CUT - FIRST], F32, name="old")
        fresh = sb.tile([P, CUT - FIRST], F32, name="fresh")
        opening = sb.tile([P, FIRST], F32, name="opening")

        def multiply(acc, i, a, b):
            nc.tensor.matmul_mx(
                out=acc,
                lhsT=w_words[i][:].bitcast(FP4X4),
                lhsT_scale=w_scales[:, i * N : (i + 1) * N],
                rhs=codes(a, b),
                rhs_scale=scales[:, a:b],
                start=True,
                stop=True,
            )

        def candidate(acc, a, b):
            nc.scalar.activation(out=cand[:, a:b], in_=acc, func=ACT.Tanh)

        def gate(acc, a, b):
            nc.scalar.activation(out=keep[:, a:b], in_=acc, func=ACT.Sigmoid, scale=-1.0)

        def product(i, a, b):
            acc = ps.tile([P, b - a], F32, name="acc%d_%d" % (i, a))
            multiply(acc[:], i, a, b)
            (candidate, gate)[i](acc[:], a, b)

        weave(1, 256, 512)
        quantise(0, 256)
        weave(1, 512, 768)
        quantise(256, 512)
        weave(1, 768, 1024)
        quantise(512, 768)
        product(0, 0, FIRST)
        nc.scalar.activation(out=old[:], in_=memory[:].indirect(entries(slot_sb, FIRST, CUT)), func=ACT.Copy)
        product(1, 0, FIRST)
        for a, b in PIECES[:2]:
            shared = ps.tile([P, 512], F32, name="shared%d" % a)
            multiply(shared[:, 256:512], 1, a, b)
            multiply(shared[:, 0:256], 0, a, b)
            candidate(shared[:, 0:256], a, b)
            gate(shared[:, 256:512], a, b)

        half = FIRST // 2
        halves = (slice(0, half), slice(half, FIRST))
        diffs = [sb.tile([P, half], F32, name="diff%d" % h.start, align_bytes=64) for h in halves]
        for diff, h in zip(diffs, halves):
            nc.vector.tensor_tensor(diff[:], memory[:].indirect(entries(slot_sb, h.start, h.stop)), cand[:, h], ALU.subtract)
        for diff, h in zip(diffs, halves):
            nc.vector.tensor_tensor(step[:, h], diff[:], keep[:, h], ALU.mult)
        for h in halves:
            nc.vector.tensor_tensor(opening[:, h], step[:, h], cand[:, h], ALU.add)
        nc.scalar.activation(out=memory[:].indirect(entries(slot_sb, 0, FIRST)), in_=opening[:], func=ACT.Copy)

        codes_sb[LATE] = sb.tile([P, S - LATE], U32, name="diff%d" % half, align_bytes=64)
        quantise(LATE, S)
        product(0, LATE, S)
        old_late = sb.tile([P, S - CUT], F32, name="opening")
        nc.scalar.activation(out=old_late[:], in_=lookup[:].indirect(entries(slot_sb, CUT, S)), func=ACT.Copy)
        product(1, LATE, S)

        middle = sb.tile([P, CUT - FIRST], F32, name="middle")
        diff = sb.tile([P, S - CUT], F32, name="diff_late")
        steps = ((FIRST, 512), (512, CUT))
        for a, b in steps:
            nc.vector.tensor_tensor(middle[:, a - FIRST : b - FIRST], old[:, a - FIRST : b - FIRST], cand[:, a:b], ALU.subtract)
        for a, b in steps:
            nc.vector.tensor_tensor(step[:, a:b], middle[:, a - FIRST : b - FIRST], keep[:, a:b], ALU.mult)
        for a, b in steps:
            nc.vector.tensor_tensor(fresh[:, a - FIRST : b - FIRST], step[:, a:b], cand[:, a:b], ALU.add)
        nc.vector.tensor_copy(out=memory[:].indirect(entries(slot_sb, FIRST, CUT)), in_=fresh[:])

        nc.gpsimd.tensor_tensor(diff[:], old_late[:], cand[:, CUT:S], ALU.subtract)
        nc.gpsimd.tensor_tensor(step[:, CUT:S], diff[:], keep[:, CUT:S], ALU.mult)
        nc.vector.tensor_tensor(memory[:].indirect(entries(slot_sb, CUT, S)), step[:, CUT:S], cand[:, CUT:S], ALU.add)
        nc.sync.dma_start(out=out, in_=memory[:])
